import numpy as np
import ml_dtypes


def mxq(x, axis, fmt="e4m3"):
    dtype, down = {"e4m3": (ml_dtypes.float8_e4m3fn, 7), "e5m2": (ml_dtypes.float8_e5m2, 14)}[fmt]
    v = np.moveaxis(np.asarray(x, np.float32).astype(ml_dtypes.bfloat16).astype(np.float64), axis, -1)
    blocks = v.reshape(v.shape[:-1] + (-1, 32))
    amax = np.abs(blocks).max(-1, keepdims=True)
    byte = np.maximum(np.where(amax > 0, np.frexp(amax)[1] - 1 + 127, 0) - down, 1)
    scale = np.exp2(byte - 127.0)
    codes = (blocks / scale).astype(np.float32).astype(dtype).astype(np.float64)
    return np.moveaxis((codes * scale).reshape(v.shape), -1, axis)


WIDE = False


def mx_kscale(k):
    if not WIDE:
        return np.ones(k)
    levels = np.array([10, -10, 5, -5, 0])
    if k % 512:
        return np.exp2(np.random.permutation(np.resize(levels, k // 32))).repeat(32)
    a = np.empty((k // 512, 16))
    for p in range(k // 512):
        a[p, :8] = np.random.permutation(np.resize(levels, 8))
        for g in range(8):
            far = levels[np.abs(levels - a[p, g]) >= 10]
            a[p, g + 8] = far[np.random.randint(len(far))]
    return np.exp2(a.ravel()).repeat(32)


BF16 = ml_dtypes.bfloat16


def bf(x):
    return np.asarray(x, np.float32).astype(BF16)


def f64(x):
    return np.asarray(x).astype(np.float64)


Q, K, D, F = 1024, 1024, 512, 1024


def draw0():
    s, t = mx_kscale(D), mx_kscale(F)
    return {"x": bf(np.random.standard_normal((Q, D)) * s),
            "y": bf(np.random.standard_normal((K, D)) * s),
            "w": bf(np.random.standard_normal((D, F)) / np.sqrt(D) / s[:, None]),
            "role": bf(np.random.uniform(-np.pi, np.pi, F)),
            "a": bf((1.0 + 0.1 * np.random.standard_normal(F)) * t),
            "c": bf((1.0 + 0.1 * np.random.standard_normal(F)) / t)}


def phasor_parts(amplitude, phase):
    return amplitude[None, :] * np.cos(phase), amplitude[None, :] * np.sin(phase)


def core(x, y, w, role, a, c):
    f = w.shape[1]
    wq = mxq(f64(w), 0, "e4m3")
    theta = mxq(f64(x), 1, "e4m3") @ wq
    phi = (mxq(f64(y), 1, "e4m3") @ wq) + f64(role)[None, :]
    qre, qim = phasor_parts(f64(a), theta)
    kre, kim = phasor_parts(f64(c), phi)
    re = mxq(qre, 1, "e4m3") @ mxq(kre, 1, "e4m3").T
    im = mxq(qim, 1, "e4m3") @ mxq(kim, 1, "e4m3").T
    return (re + im) / np.sqrt(f)


def e4m3fn_bytes(y):
    return np.clip(np.asarray(y, np.float64), -448.0, 448.0).astype(np.float32).astype(ml_dtypes.float8_e4m3fn).view(np.uint8)


def e4m3fn_values(b):
    return np.asarray(b, np.uint8).view(ml_dtypes.float8_e4m3fn).astype(np.float64)


def setup_inputs():
    d = draw0()
    x0 = np.asarray(d['y']).astype(np.float64)
    s = (np.max(np.abs(x0), axis=(0,), keepdims=True) / 448.0).astype(np.float32)
    out = {}
    for k, v in d.items():
        if k == 'y':
            out['y_bytes'] = e4m3fn_bytes(x0 / s.astype(np.float64))
            out['y_scale'] = s
        else:
            out[k] = v
    return out


def reference(x, y_bytes, y_scale, w, role, a, c):
    return core(x, e4m3fn_values(y_bytes) * y_scale.astype(np.float64), w, role, a, c)

@@ -1,0 +1,394 @@
+import math
+from contextlib import ExitStack
+
+import concourse.mybir as mybir
+from concourse.masks import make_identity
+
+Q, K, D, F = 1024, 1024, 512, 1024
+FLOPS = 2 * (Q * D * F + K * D * F + 2 * Q * K * F)
+
+F32 = mybir.dt.float32
+BF16 = mybir.dt.bfloat16
+I32 = mybir.dt.int32
+U32 = mybir.dt.uint32
+U8 = mybir.dt.uint8
+FP8 = mybir.dt.float8_e4m3fn
+FP8X4 = mybir.dt.float8_e4m3fn_x4
+ALU = mybir.AluOpType
+ACT = mybir.ActivationFunctionType
+
+P = 128
+PACK = 4
+BANK = 512
+PASSES = F // (P * PACK)
+REP = 32
+PHASE_BANKS = 4
+OTHER_BANKS = 4
+TWO_PI = 2.0 * math.pi
+
+
+def tile_fhrrbounditemsimilarity_kernel(tc, x, y_bytes, y_scale, w, role, a, c, out):
+    nc = tc.nc
+    with ExitStack() as ctx:
+        keep = ctx.enter_context(tc.tile_pool(name="keep", bufs=1))
+        work = ctx.enter_context(tc.tile_pool(name="work", bufs=2))
+        psum = ctx.enter_context(tc.psum_pool(name="psum", bufs=1))
+        ctx.enter_context(tc.manual_schedule())
+
+        def kept(name, width, dtype):
+            return keep.tile([P, width], dtype, name=name, align_bytes=64)
+
+        w_raw = [kept("w_raw%d" % g, PACK * BANK, BF16) for g in range(PASSES)]
+        x_raw = [kept("x_raw%d" % i, 2 * D, BF16) for i in range(4)]
+        y_raw = [kept("y_raw%d" % h, 4 * D, U8) for h in range(2)]
+
+        def load_w(g):
+            nc.sync.dma_start(
+                out=w_raw[g][:].rearrange("p (j f) -> p j f", j=PACK),
+                in_=w[:, g * BANK : (g + 1) * BANK].rearrange("(p j) f -> p j f", j=PACK),
+            )
+
+        def load_x(i):
+            nc.sync.dma_start(
+                out=x_raw[i][:].rearrange("p (b d) -> p b d", b=2),
+                in_=x[i * 256 : (i + 1) * 256, :].rearrange("(b p) d -> p b d", p=P),
+            )
+
+        def load_y(h):
+            nc.sync.dma_start(
+                out=y_raw[h][:].rearrange("p (b d) -> p b d", b=4),
+                in_=y_bytes[h * 512 : (h + 1) * 512, :].rearrange("(b p) d -> p b d", p=P),
+            )
+
+        load_w(0)
+        load_x(0)
+        load_y(0)
+        load_w(1)
+        load_y(1)
+        for i in range(1, 4):
+            load_x(i)
+
+        ident = kept("ident", P, F32)
+        make_identity(nc, ident[:])
+        y_sc = kept("y_sc", PACK, F32)
+        nc.gpsimd.dma_start(out=y_sc[:], in_=y_scale.rearrange("o (p t) -> p (o t)", t=PACK))
+        vec16 = {}
+        for name, vec in (("role", role), ("a", a), ("c", c)):
+            vec16[name] = kept(name + "16", PASSES * PACK, BF16)
+            nc.gpsimd.dma_start(
+                out=vec16[name][:].rearrange("p (g t) -> p g t", t=PACK),
+                in_=vec.rearrange("(g p t) -> p g t", p=P, t=PACK),
+            )
+
+        w_grp = [kept("w_grp%d" % g, PACK * BANK, BF16) for g in range(PASSES)]
+        x_grp = [kept("x_grp%d" % i, PACK * 256, BF16) for i in range(4)]
+        y_wide = [kept("y_wide%d" % h, 4 * D, BF16) for h in range(2)]
+        y_grp = [kept("y_grp%d" % h, PACK * 512, BF16) for h in range(2)]
+        mx = {}
+
+        def quantize(name, grouped):
+            width = grouped.shape[1] // PACK
+            codes = kept(name + "_codes", width, U32)
+            scales = kept(name + "_scales", width, U8)
+            nc.vector.quantize_mx(out=codes[:].bitcast(FP8X4), scales=scales[:], in_=grouped)
+            mx[name] = (codes, scales)
+
+        def operand(name, start, width):
+            codes, scales = mx[name]
+            return codes[:, start : start + width].bitcast(FP8X4), scales[:, start : start + width]
+
+        def group_w(g, copy):
+            copy(
+                out=w_grp[g][:].rearrange("p (t m j) -> p m t j", t=PACK, j=PACK),
+                in_=w_raw[g][:].rearrange("p (j m t) -> p m t j", j=PACK, t=PACK),
+            )
+
+        other_count = [0]
+
+        def other_bank():
+            n = other_count[0] % OTHER_BANKS
+            other_count[0] = other_count[0] + 1
+            return psum.tile([P, BANK], F32, name="other%d" % n)
+
+        def turn(rows, first):
+            words = rows[:].bitcast(F32)
+            bank = other_bank()
+            for b in range(2):
+                for u in range(2):
+                    lo = (first + b) * 256
+                    nc.tensor.transpose(
+                        bank[:, u * 256 + b * P : u * 256 + (b + 1) * P], words[:, lo + u : lo + 256 : 2], ident[:]
+                    )
+            return bank
+
+        def group_x(i):
+            bank = turn(x_raw[i], 0)
+            nc.scalar.copy(
+                out=x_grp[i][:].bitcast(F32).rearrange("p (r u) -> p r u", u=2),
+                in_=bank[:].rearrange("p (u r) -> p r u", u=2),
+            )
+
+        def widen_y(h):
+            nc.scalar.copy(out=y_wide[h][:], in_=y_raw[h][:].bitcast(FP8))
+
+        def scale_y(h, half, bank):
+            nc.vector.tensor_tensor(
+                out=y_grp[h][:, half * 1024 : (half + 1) * 1024].rearrange("p (r u e) -> p r u e", u=2, e=2),
+                in0=bank[:].bitcast(BF16).rearrange("p (u r e) -> p r u e", u=2, e=2),
+                in1=y_sc[:].rearrange("p (u e) -> p u e", u=2).unsqueeze(1).broadcast_to([P, 256, 2, 2]),
+                op=ALU.mult,
+            )
+
+        role32 = kept("role32", PASSES * PACK, F32)
+        rep = {"a": kept("a_rep", PASSES * REP * PACK, F32), "c": kept("c_rep", PASSES * REP * PACK, F32)}
+
+        def spread(name):
+            nc.vector.tensor_copy(
+                out=rep[name][:].rearrange("p (g r t) -> p g r t", g=PASSES, t=PACK),
+                in_=vec16[name][:].rearrange("p (g t) -> p g t", t=PACK).unsqueeze(2).broadcast_to([P, PASSES, REP, PACK]),
+            )
+
+        chunks = [("q", 0, 256)] + [("k", h, g) for h in range(2) for g in range(PASSES)]
+        chunks = chunks + [("q", 256, 256), ("q", 512, 256), ("q", 768, 128), ("q", 896, 128)]
+
+        def columns(s):
+            side, first, n = chunks[s]
+            return PASSES * PACK * n if side == "q" else PACK * BANK
+
+        banks = [(s, b) for s in range(len(chunks)) for b in range(columns(s) // BANK)]
+        first_bank = [banks.index((s, 0)) for s in range(len(chunks))]
+        phase = {}
+        turns = {}
+        reduced = {}
+        state = {"mm": 0, "done": 0}
+
+        def phase_matmul(n):
+            s, b = banks[n]
+            side, first, third = chunks[s]
+            bank = psum.tile([P, BANK], F32, name="phase%d" % (n % PHASE_BANKS))
+            phase[n] = bank
+            if side == "q":
+                g, j = divmod(b, third // P)
+                block = first // P + j
+                rhs, rhs_scale = operand("x%d" % (block // 2), (block % 2) * P, P)
+                for t in range(PACK):
+                    lhsT, lhsT_scale = operand("w%d" % g, t * P, P)
+                    nc.tensor.matmul_mx(out=bank[:, t * P : (t + 1) * P], lhsT=lhsT, lhsT_scale=lhsT_scale,
+                                        rhs=rhs, rhs_scale=rhs_scale, start=True, stop=True)
+            else:
+                rhs, rhs_scale = operand("y%d" % first, 0, BANK)
+                lhsT, lhsT_scale = operand("w%d" % third, b * P, P)
+                nc.tensor.matmul_mx(out=bank[:], lhsT=lhsT, lhsT_scale=lhsT_scale,
+                                    rhs=rhs, rhs_scale=rhs_scale, start=True, stop=True)
+
+        def ready(n):
+            s, b = banks[n]
+            side, first, third = chunks[s]
+            if side == "q":
+                g, j = divmod(b, third // P)
+                return "w%d" % g in mx and "x%d" % ((first // P + j) // 2) in mx
+            return "w%d" % third in mx and "y%d" % first in mx
+
+        def pump():
+            while state["mm"] < min(len(banks), state["done"] + PHASE_BANKS) and ready(state["mm"]):
+                phase_matmul(state["mm"])
+                state["mm"] = state["mm"] + 1
+
+        def phase_view(n, ap):
+            if chunks[banks[n][0]][0] == "q":
+                return ap.rearrange("p (n t) -> p n t", t=PACK)
+            return ap
+
+        def bank_view(n):
+            if chunks[banks[n][0]][0] == "q":
+                return phase[n][:].rearrange("p (t n) -> p n t", t=PACK)
+            return phase[n][:]
+
+        def count_turns(n):
+            s, b = banks[n]
+            side, first, third = chunks[s]
+            turns[n] = work.tile([P, BANK], I32, name="turns", bufs=3, align_bytes=64)
+            if side == "q":
+                nc.vector.tensor_scalar(out=phase_view(n, turns[n][:]), in0=bank_view(n), scalar1=1.0 / TWO_PI,
+                                        scalar2=None, op0=ALU.mult)
+            else:
+                col = third * PACK + b
+                nc.vector.tensor_scalar(out=turns[n][:], in0=bank_view(n), scalar1=role32[:, col : col + 1],
+                                        scalar2=1.0 / TWO_PI, op0=ALU.add, op1=ALU.mult)
+
+        def subtract_turns(n):
+            s, b = banks[n]
+            if b == 0:
+                reduced[s] = work.tile([P, columns(s)], F32, name="reduced", bufs=2, align_bytes=64)
+            nc.vector.scalar_tensor_tensor(
+                out=phase_view(n, reduced[s][:, b * BANK : (b + 1) * BANK]), in0=phase_view(n, turns[n][:]),
+                scalar=-TWO_PI, in1=bank_view(n), op0=ALU.mult, op1=ALU.add)
+            state["done"] = n + 1
+            pump()
+
+        def reduce_banks(lo, hi):
+            count_turns(lo)
+            for n in range(lo, hi):
+                if n + 1 < hi:
+                    count_turns(n + 1)
+                subtract_turns(n)
+
+        def reduce_chunk(s):
+            reduce_banks(first_bank[s], first_bank[s] + columns(s) // BANK)
+
+        cosines, sines = {}, {}
+
+        def trig(s, lo, hi):
+            side, first, third = chunks[s]
+            if lo == 0:
+                cosines[s] = work.tile([P, columns(s)], F32, name="cosines", bufs=3, align_bytes=64)
+                sines[s] = work.tile([P, columns(s)], F32, name="sines", bufs=3, align_bytes=64)
+            folded = work.tile([P, hi - lo], F32, name="folded", bufs=2, align_bytes=64)
+            if side == "q":
+                nc.scalar.activation(out=sines[s][:, lo:hi], in_=reduced[s][:, lo:hi], func=ACT.Sin)
+                nc.scalar.activation(out=folded[:], in_=reduced[s][:, lo:hi], func=ACT.Abs)
+                nc.scalar.activation(out=cosines[s][:, lo:hi], in_=folded[:], func=ACT.Sin, scale=-1.0, bias=math.pi / 2)
+            else:
+                for func, dst in ((ACT.Abs, folded), (ACT.Sin, sines[s])):
+                    for t in range(PACK):
+                        col = third * PACK + t
+                        nc.scalar.activation(out=dst[:, t * BANK : (t + 1) * BANK],
+                                             in_=reduced[s][:, t * BANK : (t + 1) * BANK],
+                                             func=func, bias=role32[:, col : col + 1])
+                nc.scalar.activation(
+                    out=cosines[s][:].rearrange("p (m i t) -> p m t i", i=2, t=PACK),
+                    in_=folded[:].rearrange("p (t m i) -> p m t i", i=2, t=PACK),
+                    func=ACT.Sin, scale=-1.0, bias=math.pi / 2)
+
+        parts = {}
+
+        def times_amplitude(engine, s, src, base, lo, hi):
+            side, first, third = chunks[s]
+            width = columns(s)
+            groups = PASSES if side == "q" else 1
+            amp = rep["a"][:] if side == "q" else rep["c"][:, third * REP * PACK : (third + 1) * REP * PACK]
+            runs = (hi - lo) // REP
+
+            def view(ap):
+                ap = ap.rearrange("p (g f) -> p g f", g=groups)[:, :, lo * PACK : hi * PACK]
+                return ap.rearrange("p g (n f) -> p g n f", f=REP * PACK)
+
+            engine.tensor_tensor(
+                out=view(parts[s][:, base : base + width]), in0=view(src[:]),
+                in1=amp.rearrange("p (g f) -> p g f", g=groups).unsqueeze(2).broadcast_to([P, groups, runs, REP * PACK]),
+                op=ALU.mult)
+
+        def tokens(s):
+            return chunks[s][2] if chunks[s][0] == "q" else BANK
+
+        def real_on_gpsimd(s, share):
+            parts[s] = work.tile([P, 2 * columns(s)], BF16, name="parts", bufs=1, align_bytes=64)
+            if share:
+                times_amplitude(nc.gpsimd, s, cosines[s], 0, 0, share)
+
+        def rest_on_vector(s, share):
+            side, first, third = chunks[s]
+            width = columns(s)
+            if side == "q":
+                times_amplitude(nc.vector, s, sines[s], width, 0, tokens(s))
+            else:
+                lo = third * REP * PACK
+                nc.vector.tensor_tensor(
+                    out=parts[s][:, width : 2 * width].rearrange("p (m i t) -> p m t i", i=2, t=PACK),
+                    in0=sines[s][:].rearrange("p (t m i) -> p m t i", i=2, t=PACK),
+                    in1=rep["c"][:, lo : lo + PACK].unsqueeze(1).unsqueeze(3).broadcast_to([P, BANK // 2, PACK, 2]),
+                    op=ALU.mult)
+            if share < tokens(s):
+                times_amplitude(nc.vector, s, cosines[s], 0, share, tokens(s))
+
+        def products(s):
+            found = []
+            for sq in range(s + 1):
+                if chunks[sq][0] != "q":
+                    continue
+                for h in range(2):
+                    last = max(sq, chunks.index(("k", h, PASSES - 1)))
+                    if last == s:
+                        found.extend((sq, j, h) for j in range(chunks[sq][2] // P))
+            return found
+
+        def similarity(job):
+            sq, j, h = job
+            n = chunks[sq][2]
+            bank = other_bank()
+            steps = [(part, g) for part in range(2) for g in range(PASSES)]
+            for part, g in steps:
+                lhsT, lhsT_scale = operand("chunk%d" % sq, (part * PASSES + g) * n + j * P, P)
+                rhs, rhs_scale = operand("chunk%d" % chunks.index(("k", h, g)), part * BANK, BANK)
+                nc.tensor.matmul_mx(out=bank[:], lhsT=lhsT, lhsT_scale=lhsT_scale, rhs=rhs, rhs_scale=rhs_scale,
+                                    start=(part, g) == steps[0], stop=(part, g) == steps[-1])
+            return bank
+
+        def store(job, bank, on_vector):
+            sq, j, h = job
+            row = chunks[sq][1] + j * P
+            result = work.tile([P, BANK], F32, name="result", bufs=4, align_bytes=64)
+            if on_vector:
+                nc.vector.tensor_scalar(out=result[:], in0=bank[:], scalar1=1.0 / math.sqrt(F), scalar2=None, op0=ALU.mult)
+            else:
+                nc.scalar.activation(out=result[:], in_=bank[:], func=ACT.Copy, scale=1.0 / math.sqrt(F))
+            nc.sync.dma_start(out=out[row : row + P, h * BANK : (h + 1) * BANK], in_=result[:])
+
+        group_w(0, nc.vector.tensor_copy)
+        group_x(0)
+        widen_y(0)
+        quantize("w0", w_grp[0][:])
+        quantize("x0", x_grp[0][:])
+        pump()
+        y_banks = [turn(y_wide[0], 0), turn(y_wide[0], 2)]
+        group_w(1, nc.scalar.copy)
+        reduce_banks(0, 2)
+        scale_y(0, 0, y_banks[0])
+        scale_y(0, 1, y_banks[1])
+        quantize("w1", w_grp[1][:])
+        pump()
+        trig(0, 0, 1024)
+        widen_y(1)
+        quantize("y0", y_grp[0][:])
+        pump()
+        nc.vector.tensor_copy(out=role32[:], in_=vec16["role"][:])
+        spread("a")
+        spread("c")
+        reduce_banks(2, 4)
+        trig(0, 1024, 2048)
+        y_banks = [turn(y_wide[1], 0), turn(y_wide[1], 2)]
+        group_x(1)
+        group_x(2)
+        reduce_chunk(1)
+        trig(1, 0, columns(1))
+
+        pending = []
+        for s in range(len(chunks)):
+            ahead = s + 2
+            window = columns(ahead) if ahead < len(chunks) else 0
+            per_token = columns(s) // tokens(s)
+            share = tokens(s) if s == 0 else (window * 7 // 8 // per_token) // REP * REP
+            share = min(share, tokens(s))
+            real_on_gpsimd(s, share)
+            if window:
+                reduce_chunk(ahead)
+            if s == 0:
+                scale_y(1, 0, y_banks[0])
+                scale_y(1, 1, y_banks[1])
+                group_x(3)
+            for job, bank in pending:
+                store(job, bank, False)
+            if window:
+                trig(ahead, 0, columns(ahead))
+            rest_on_vector(s, share)
+            if s == 0:
+                quantize("y1", y_grp[1][:])
+                pump()
+            if s == 1:
+                for i in range(1, 4):
+                    quantize("x%d" % i, x_grp[i][:])
+            quantize("chunk%d" % s, parts[s][:])
+            pump()
+            pending = [(job, similarity(job)) for job in products(s)]
+        for n, (job, bank) in enumerate(pending):
+            store(job, bank, n % 2 == 1)

@@ -23,7 +23,7 @@ BANK = 512
 PASSES = F // (P * PACK)
 REP = 32
 PHASE_BANKS = 4
-OTHER_BANKS = 4
+OTHER_BANKS = 3
 TWO_PI = 2.0 * math.pi
 
 
@@ -80,6 +80,10 @@ def tile_fhrrbounditemsimilarity_kernel(tc, x, y_bytes, y_scale, w, role, a, c, 
                 in_=vec.rearrange("(g p t) -> p g t", p=P, t=PACK),
             )
 
+        ident16 = kept("ident16", P, BF16)
+        make_identity(nc, ident16[:])
+        amp_bank = psum.tile([P, BANK], F32, name="amp_bank")
+
         w_grp = [kept("w_grp%d" % g, PACK * BANK, BF16) for g in range(PASSES)]
         x_grp = [kept("x_grp%d" % i, PACK * 256, BF16) for i in range(4)]
         y_wide = [kept("y_wide%d" % h, 4 * D, BF16) for h in range(2)]
@@ -103,16 +107,19 @@ def tile_fhrrbounditemsimilarity_kernel(tc, x, y_bytes, y_scale, w, role, a, c, 
                 in_=w_raw[g][:].rearrange("p (j m t) -> p m t j", j=PACK, t=PACK),
             )
 
-        other_count = [0]
+        free_banks = ["other%d" % n for n in range(OTHER_BANKS)]
+        bank_number = {}
 
-        def other_bank():
-            n = other_count[0] % OTHER_BANKS
-            other_count[0] = other_count[0] + 1
-            return psum.tile([P, BANK], F32, name="other%d" % n)
+        def take_bank(user):
+            bank_number[user] = free_banks.pop(0)
+            return psum.tile([P, BANK], F32, name=bank_number[user])
 
-        def turn(rows, first):
+        def give_bank(user):
+            free_banks.append(bank_number[user])
+
+        def turn(user, rows, first):
             words = rows[:].bitcast(F32)
-            bank = other_bank()
+            bank = take_bank(user)
             for b in range(2):
                 for u in range(2):
                     lo = (first + b) * 256
@@ -122,11 +129,12 @@ def tile_fhrrbounditemsimilarity_kernel(tc, x, y_bytes, y_scale, w, role, a, c, 
             return bank
 
         def group_x(i):
-            bank = turn(x_raw[i], 0)
+            bank = turn(("x", i), x_raw[i], 0)
             nc.scalar.copy(
                 out=x_grp[i][:].bitcast(F32).rearrange("p (r u) -> p r u", u=2),
                 in_=bank[:].rearrange("p (u r) -> p r u", u=2),
             )
+            give_bank(("x", i))
 
         def widen_y(h):
             nc.scalar.copy(out=y_wide[h][:], in_=y_raw[h][:].bitcast(FP8))
@@ -138,6 +146,7 @@ def tile_fhrrbounditemsimilarity_kernel(tc, x, y_bytes, y_scale, w, role, a, c, 
                 in1=y_sc[:].rearrange("p (u e) -> p u e", u=2).unsqueeze(1).broadcast_to([P, 256, 2, 2]),
                 op=ALU.mult,
             )
+            give_bank(("y", h, half))
 
         role32 = kept("role32", PASSES * PACK, F32)
         rep = {"a": kept("a_rep", PASSES * REP * PACK, F32), "c": kept("c_rep", PASSES * REP * PACK, F32)}
@@ -148,12 +157,14 @@ def tile_fhrrbounditemsimilarity_kernel(tc, x, y_bytes, y_scale, w, role, a, c, 
                 in_=vec16[name][:].rearrange("p (g t) -> p g t", t=PACK).unsqueeze(2).broadcast_to([P, PASSES, REP, PACK]),
             )
 
-        chunks = [("q", 0, 256)] + [("k", h, g) for h in range(2) for g in range(PASSES)]
-        chunks = chunks + [("q", 256, 256), ("q", 512, 256), ("q", 768, 128), ("q", 896, 128)]
+        both = list(range(PASSES))
+        chunks = [("q", 0, 256, [g]) for g in both]
+        chunks = chunks + [("k", h * BANK, BANK, [g]) for h in range(2) for g in both]
+        for count in (256, 256, 128, 128):
+            chunks = chunks + [("q", 256 + sum(ch[2] for ch in chunks[6:]), count, both)]
 
         def columns(s):
-            side, first, n = chunks[s]
-            return PASSES * PACK * n if side == "q" else PACK * BANK
+            return PACK * chunks[s][2] * len(chunks[s][3])
 
         banks = [(s, b) for s in range(len(chunks)) for b in range(columns(s) // BANK)]
         first_bank = [banks.index((s, 0)) for s in range(len(chunks))]
@@ -162,35 +173,35 @@ def tile_fhrrbounditemsimilarity_kernel(tc, x, y_bytes, y_scale, w, role, a, c, 
         reduced = {}
         state = {"mm": 0, "done": 0}
 
+        def bank_operands(n):
+            s, b = banks[n]
+            side, first, count, passes = chunks[s]
+            if side == "q":
+                g, j = divmod(b, count // P)
+                block = first // P + j
+                return "w%d" % passes[g], "x%d" % (block // 2), (block % 2) * P
+            return "w%d" % passes[0], "y%d" % (first // BANK), 0
+
         def phase_matmul(n):
             s, b = banks[n]
-            side, first, third = chunks[s]
             bank = psum.tile([P, BANK], F32, name="phase%d" % (n % PHASE_BANKS))
             phase[n] = bank
-            if side == "q":
-                g, j = divmod(b, third // P)
-                block = first // P + j
-                rhs, rhs_scale = operand("x%d" % (block // 2), (block % 2) * P, P)
-                for t in range(PACK):
-                    lhsT, lhsT_scale = operand("w%d" % g, t * P, P)
-                    nc.tensor.matmul_mx(out=bank[:, t * P : (t + 1) * P], lhsT=lhsT, lhsT_scale=lhsT_scale,
-                                        rhs=rhs, rhs_scale=rhs_scale, start=True, stop=True)
+            weights, rows, start = bank_operands(n)
+            if chunks[s][0] == "q":
+                todo = [(t, bank[:, t * P : (t + 1) * P], P) for t in range(PACK)]
             else:
-                rhs, rhs_scale = operand("y%d" % first, 0, BANK)
-                lhsT, lhsT_scale = operand("w%d" % third, b * P, P)
-                nc.tensor.matmul_mx(out=bank[:], lhsT=lhsT, lhsT_scale=lhsT_scale,
-                                    rhs=rhs, rhs_scale=rhs_scale, start=True, stop=True)
-
-        def ready(n):
-            s, b = banks[n]
-            side, first, third = chunks[s]
-            if side == "q":
-                g, j = divmod(b, third // P)
-                return "w%d" % g in mx and "x%d" % ((first // P + j) // 2) in mx
-            return "w%d" % third in mx and "y%d" % first in mx
+                todo = [(b, bank[:], BANK)]
+            for t, dst, width in todo:
+                lhsT, lhsT_scale = operand(weights, t * P, P)
+                rhs, rhs_scale = operand(rows, start, width)
+                nc.tensor.matmul_mx(out=dst, lhsT=lhsT, lhsT_scale=lhsT_scale, rhs=rhs, rhs_scale=rhs_scale,
+                                    start=True, stop=True)
 
         def pump():
-            while state["mm"] < min(len(banks), state["done"] + PHASE_BANKS) and ready(state["mm"]):
+            while state["mm"] < min(len(banks), state["done"] + PHASE_BANKS):
+                weights, rows, start = bank_operands(state["mm"])
+                if weights not in mx or rows not in mx:
+                    return
                 phase_matmul(state["mm"])
                 state["mm"] = state["mm"] + 1
 
@@ -206,13 +217,13 @@ def tile_fhrrbounditemsimilarity_kernel(tc, x, y_bytes, y_scale, w, role, a, c, 
 
         def count_turns(n):
             s, b = banks[n]
-            side, first, third = chunks[s]
+            side, first, count, passes = chunks[s]
             turns[n] = work.tile([P, BANK], I32, name="turns", bufs=3, align_bytes=64)
             if side == "q":
                 nc.vector.tensor_scalar(out=phase_view(n, turns[n][:]), in0=bank_view(n), scalar1=1.0 / TWO_PI,
                                         scalar2=None, op0=ALU.mult)
             else:
-                col = third * PACK + b
+                col = passes[0] * PACK + b
                 nc.vector.tensor_scalar(out=turns[n][:], in0=bank_view(n), scalar1=role32[:, col : col + 1],
                                         scalar2=1.0 / TWO_PI, op0=ALU.add, op1=ALU.mult)
 
@@ -225,170 +236,237 @@ def tile_fhrrbounditemsimilarity_kernel(tc, x, y_bytes, y_scale, w, role, a, c, 
                 scalar=-TWO_PI, in1=bank_view(n), op0=ALU.mult, op1=ALU.add)
             state["done"] = n + 1
             pump()
+            if n + PHASE_BANKS >= len(banks):
+                free_banks.append("phase%d" % (n % PHASE_BANKS))
 
-        def reduce_banks(lo, hi):
+        def reduce_chunk(s):
+            lo, hi = first_bank[s], first_bank[s] + columns(s) // BANK
             count_turns(lo)
             for n in range(lo, hi):
                 if n + 1 < hi:
                     count_turns(n + 1)
                 subtract_turns(n)
 
-        def reduce_chunk(s):
-            reduce_banks(first_bank[s], first_bank[s] + columns(s) // BANK)
+        trigs = {}
 
-        cosines, sines = {}, {}
+        def trig(s):
+            side, first, count, passes = chunks[s]
+            cosines = work.tile([P, columns(s)], F32, name="cosines", bufs=3, align_bytes=64)
+            sines = work.tile([P, columns(s)], F32, name="sines", bufs=3, align_bytes=64)
+            folded = work.tile([P, columns(s)], F32, name="folded", bufs=2, align_bytes=64)
+            trigs[s] = (cosines, sines)
+            pieces = columns(s) // BANK
 
-        def trig(s, lo, hi):
-            side, first, third = chunks[s]
-            if lo == 0:
-                cosines[s] = work.tile([P, columns(s)], F32, name="cosines", bufs=3, align_bytes=64)
-                sines[s] = work.tile([P, columns(s)], F32, name="sines", bufs=3, align_bytes=64)
-            folded = work.tile([P, hi - lo], F32, name="folded", bufs=2, align_bytes=64)
+            def shifted(func, dst, lo, hi):
+                if side == "q":
+                    nc.scalar.activation(out=dst[:, lo * BANK : hi * BANK], in_=reduced[s][:, lo * BANK : hi * BANK], func=func)
+                    return
+                for t in range(lo, hi):
+                    col = passes[0] * PACK + t
+                    nc.scalar.activation(out=dst[:, t * BANK : (t + 1) * BANK],
+                                         in_=reduced[s][:, t * BANK : (t + 1) * BANK],
+                                         func=func, bias=role32[:, col : col + 1])
+
+            for b in range(pieces):
+                shifted(ACT.Abs, folded, b, b + 1)
+            if 1:
+                shifted(ACT.Sin, sines, 0, 1)
             if side == "q":
-                nc.scalar.activation(out=sines[s][:, lo:hi], in_=reduced[s][:, lo:hi], func=ACT.Sin)
-                nc.scalar.activation(out=folded[:], in_=reduced[s][:, lo:hi], func=ACT.Abs)
-                nc.scalar.activation(out=cosines[s][:, lo:hi], in_=folded[:], func=ACT.Sin, scale=-1.0, bias=math.pi / 2)
+                nc.scalar.activation(out=cosines[:], in_=folded[:], func=ACT.Sin, scale=-1.0, bias=math.pi / 2)
             else:
-                for func, dst in ((ACT.Abs, folded), (ACT.Sin, sines[s])):
-                    for t in range(PACK):
-                        col = third * PACK + t
-                        nc.scalar.activation(out=dst[:, t * BANK : (t + 1) * BANK],
-                                             in_=reduced[s][:, t * BANK : (t + 1) * BANK],
-                                             func=func, bias=role32[:, col : col + 1])
                 nc.scalar.activation(
-                    out=cosines[s][:].rearrange("p (m i t) -> p m t i", i=2, t=PACK),
+                    out=cosines[:].rearrange("p (m i t) -> p m t i", i=2, t=PACK),
                     in_=folded[:].rearrange("p (t m i) -> p m t i", i=2, t=PACK),
                     func=ACT.Sin, scale=-1.0, bias=math.pi / 2)
+            if pieces > 1:
+                shifted(ACT.Sin, sines, 1, pieces)
 
         parts = {}
 
-        def times_amplitude(engine, s, src, base, lo, hi):
-            side, first, third = chunks[s]
+        def times_amplitude(on_gpsimd, s, lo, hi):
+            side, first, count, passes = chunks[s]
+            while lo < hi:
+                segment, token = divmod(lo, count)
+                part, g = divmod(segment, len(passes))
+                if token == 0 and g == 0 and hi - lo >= count * len(passes):
+                    groups, rows = len(passes), count
+                else:
+                    groups, rows = 1, min(count - token, hi - lo)
+                product(on_gpsimd, s, part, g, groups, token, token + rows)
+                lo = lo + groups * rows
+
+        def product(on_gpsimd, s, part, g, groups, lo, hi):
+            side, first, count, passes = chunks[s]
             width = columns(s)
-            groups = PASSES if side == "q" else 1
-            amp = rep["a"][:] if side == "q" else rep["c"][:, third * REP * PACK : (third + 1) * REP * PACK]
-            runs = (hi - lo) // REP
+            run = REP * PACK
+            cols = slice(g * count * PACK, (g + groups) * count * PACK)
+            dst = parts[s][:, part * width : (part + 1) * width][:, cols]
+            src = trigs[s][part][:, cols]
+            engine = nc.gpsimd if on_gpsimd else nc.vector
+            name = "a" if side == "q" else "c"
+            amp = rep[name][:, passes[g] * run : (passes[g] + groups) * run].rearrange("p (g f) -> p g f", g=groups)
+            if not on_gpsimd:
+                base = (0 if side == "q" else PASSES * PACK) + passes[g] * PACK
+                amp = amp_bank[:, base : base + groups * PACK].rearrange("p (g f) -> p g f", g=groups)
+            if side == "k" and part == 1:
+                pairs = slice(lo // 2, hi // 2)
+                engine.tensor_tensor(
+                    out=dst.rearrange("p (m i t) -> p m t i", i=2, t=PACK)[:, pairs],
+                    in0=src.rearrange("p (t m i) -> p m t i", i=2, t=PACK)[:, pairs],
+                    in1=amp[:, 0, 0:PACK].unsqueeze(1).unsqueeze(3).broadcast_to([P, (hi - lo) // 2, PACK, 2]),
+                    op=ALU.mult)
+                return
+            inner = run if on_gpsimd else PACK
 
             def view(ap):
                 ap = ap.rearrange("p (g f) -> p g f", g=groups)[:, :, lo * PACK : hi * PACK]
-                return ap.rearrange("p g (n f) -> p g n f", f=REP * PACK)
+                return ap.rearrange("p g (n f) -> p g n f", f=inner)
 
             engine.tensor_tensor(
-                out=view(parts[s][:, base : base + width]), in0=view(src[:]),
-                in1=amp.rearrange("p (g f) -> p g f", g=groups).unsqueeze(2).broadcast_to([P, groups, runs, REP * PACK]),
+                out=view(dst), in0=view(src),
+                in1=amp.unsqueeze(2).broadcast_to([P, groups, (hi - lo) * PACK // inner, inner]),
                 op=ALU.mult)
 
-        def tokens(s):
-            return chunks[s][2] if chunks[s][0] == "q" else BANK
+        def piece(side, token, part, g, width):
+            for s, (side_s, first, count, passes) in enumerate(chunks):
+                if side_s == side and first <= token < first + count and g in passes:
+                    name = "part%d_%d" % (s, part)
+                    if name in mx:
+                        return operand(name, passes.index(g) * count + token - first, width)
+            return None
 
-        def real_on_gpsimd(s, share):
-            parts[s] = work.tile([P, 2 * columns(s)], BF16, name="parts", bufs=1, align_bytes=64)
-            if share:
-                times_amplitude(nc.gpsimd, s, cosines[s], 0, 0, share)
+        def step_of(side, token, g):
+            return [s for s, ch in enumerate(chunks) if ch[0] == side and ch[1] <= token < ch[1] + ch[2] and g in ch[3]][0]
 
-        def rest_on_vector(s, share):
-            side, first, third = chunks[s]
-            width = columns(s)
-            if side == "q":
-                times_amplitude(nc.vector, s, sines[s], width, 0, tokens(s))
-            else:
-                lo = third * REP * PACK
-                nc.vector.tensor_tensor(
-                    out=parts[s][:, width : 2 * width].rearrange("p (m i t) -> p m t i", i=2, t=PACK),
-                    in0=sines[s][:].rearrange("p (t m i) -> p m t i", i=2, t=PACK),
-                    in1=rep["c"][:, lo : lo + PACK].unsqueeze(1).unsqueeze(3).broadcast_to([P, BANK // 2, PACK, 2]),
-                    op=ALU.mult)
-            if share < tokens(s):
-                times_amplitude(nc.vector, s, cosines[s], 0, share, tokens(s))
+        jobs = [(row, col) for row in range(0, Q, P) for col in range(0, K, BANK)]
+        opens = {job: max(step_of("q", job[0], 0), step_of("k", job[1], PASSES - 1)) for job in jobs}
+        todo = {job: [(part, g) for part in (1, 0) for g in both] for job in jobs}
+        sums = {}
+        finished = []
 
-        def products(s):
-            found = []
-            for sq in range(s + 1):
-                if chunks[sq][0] != "q":
-                    continue
-                for h in range(2):
-                    last = max(sq, chunks.index(("k", h, PASSES - 1)))
-                    if last == s:
-                        found.extend((sq, j, h) for j in range(chunks[sq][2] // P))
-            return found
+        def similarity(s):
+            for job in jobs:
+                for part, g in [(part, g) for part in (1, 0) for g in both]:
+                    if opens[job] > s or (part, g) not in todo[job]:
+                        continue
+                    left, right = piece("q", job[0], part, g, P), piece("k", job[1], part, g, BANK)
+                    if left is None or right is None:
+                        continue
+                    start = job not in sums
+                    if start and not free_banks:
+                        continue
+                    if start:
+                        sums[job] = take_bank(job)
+                    todo[job].remove((part, g))
+                    nc.tensor.matmul_mx(out=sums[job][:], lhsT=left[0], lhsT_scale=left[1], rhs=right[0], rhs_scale=right[1],
+                                        start=start, stop=not todo[job])
+                    if not todo[job]:
+                        finished.append(job)
 
-        def similarity(job):
-            sq, j, h = job
-            n = chunks[sq][2]
-            bank = other_bank()
-            steps = [(part, g) for part in range(2) for g in range(PASSES)]
-            for part, g in steps:
-                lhsT, lhsT_scale = operand("chunk%d" % sq, (part * PASSES + g) * n + j * P, P)
-                rhs, rhs_scale = operand("chunk%d" % chunks.index(("k", h, g)), part * BANK, BANK)
-                nc.tensor.matmul_mx(out=bank[:], lhsT=lhsT, lhsT_scale=lhsT_scale, rhs=rhs, rhs_scale=rhs_scale,
-                                    start=(part, g) == steps[0], stop=(part, g) == steps[-1])
-            return bank
-
-        def store(job, bank, on_vector):
-            sq, j, h = job
-            row = chunks[sq][1] + j * P
+        def store(s, job, on_vector):
+            row, col = job
             result = work.tile([P, BANK], F32, name="result", bufs=4, align_bytes=64)
             if on_vector:
-                nc.vector.tensor_scalar(out=result[:], in0=bank[:], scalar1=1.0 / math.sqrt(F), scalar2=None, op0=ALU.mult)
+                nc.vector.tensor_scalar(out=result[:], in0=sums[job][:], scalar1=1.0 / math.sqrt(F), scalar2=None, op0=ALU.mult)
             else:
-                nc.scalar.activation(out=result[:], in_=bank[:], func=ACT.Copy, scale=1.0 / math.sqrt(F))
-            nc.sync.dma_start(out=out[row : row + P, h * BANK : (h + 1) * BANK], in_=result[:])
+                nc.scalar.activation(out=result[:], in_=sums[job][:], func=ACT.Copy, scale=1.0 / math.sqrt(F))
+            nc.sync.dma_start(out=out[row : row + P, col : col + BANK], in_=result[:])
+            give_bank(job)
+            finished.remove(job)
+            similarity(s)
 
+        warm = kept("warm", 1, F32)
+        nc.vector.memset(warm[:], 0.0)
+        nc.scalar.activation(out=warm[:], in_=warm[:], func=ACT.Sin)
         group_w(0, nc.vector.tensor_copy)
         group_x(0)
         widen_y(0)
         quantize("w0", w_grp[0][:])
         quantize("x0", x_grp[0][:])
         pump()
-        y_banks = [turn(y_wide[0], 0), turn(y_wide[0], 2)]
+        y_banks = [turn(("y", 0, half), y_wide[0], 2 * half) for half in range(2)]
         group_w(1, nc.scalar.copy)
-        reduce_banks(0, 2)
+        reduce_chunk(0)
         scale_y(0, 0, y_banks[0])
         scale_y(0, 1, y_banks[1])
         quantize("w1", w_grp[1][:])
         pump()
-        trig(0, 0, 1024)
+        trig(0)
         widen_y(1)
         quantize("y0", y_grp[0][:])
         pump()
+        for n, name in enumerate(("a", "c")):
+            nc.tensor.matmul(out=amp_bank[:, n * PASSES * PACK : (n + 1) * PASSES * PACK], lhsT=ident16[:],
+                             rhs=vec16[name][:], start=True, stop=True)
         nc.vector.tensor_copy(out=role32[:], in_=vec16["role"][:])
         spread("a")
         spread("c")
-        reduce_banks(2, 4)
-        trig(0, 1024, 2048)
-        y_banks = [turn(y_wide[1], 0), turn(y_wide[1], 2)]
-        group_x(1)
-        group_x(2)
         reduce_chunk(1)
-        trig(1, 0, columns(1))
+        trig(1)
+        y_banks = [turn(("y", 1, half), y_wide[1], 2 * half) for half in range(2)]
+        parts[0] = work.tile([P, 2 * columns(0)], BF16, name="parts_first", bufs=1, align_bytes=64)
+        times_amplitude(True, 0, 0, 2 * chunks[0][2])
+        reduce_chunk(2)
+        trig(2)
+        parts[1] = work.tile([P, 2 * columns(1)], BF16, name="parts_second", bufs=1, align_bytes=64)
+        times_amplitude(True, 1, 0, 2 * chunks[1][2])
+        made = 3
+        if 1:
+            parts[2] = work.tile([P, 2 * columns(2)], BF16, name="parts", bufs=1, align_bytes=64)
+            times_amplitude(True, 2, 0, 512)
+        reduce_chunk(3)
+        scale_y(1, 0, y_banks[0])
+        scale_y(1, 1, y_banks[1])
+        trig(3)
+        group_x(1)
+        if 1:
+            times_amplitude(False, 2, 512, 2 * BANK)
+        quantize("y1", y_grp[1][:])
+        pump()
+        for done in range(2 + 1):
+            for part in (0, 1):
+                quantize("part%d_%d" % (done, part), parts[done][:, part * columns(done) : (part + 1) * columns(done)])
+        made = 4
 
-        pending = []
-        for s in range(len(chunks)):
-            ahead = s + 2
-            window = columns(ahead) if ahead < len(chunks) else 0
-            per_token = columns(s) // tokens(s)
-            share = tokens(s) if s == 0 else (window * 7 // 8 // per_token) // REP * REP
-            share = min(share, tokens(s))
-            real_on_gpsimd(s, share)
-            if window:
-                reduce_chunk(ahead)
-            if s == 0:
-                scale_y(1, 0, y_banks[0])
-                scale_y(1, 1, y_banks[1])
-                group_x(3)
-            for job, bank in pending:
-                store(job, bank, False)
-            if window:
-                trig(ahead, 0, columns(ahead))
-            rest_on_vector(s, share)
-            if s == 0:
-                quantize("y1", y_grp[1][:])
+        for s in range(2 + 1, len(chunks)):
+            side, first, count, passes = chunks[s]
+            lag = 1 if s < 6 else 2
+            ahead = list(range(made, min(s + lag + 1, len(chunks))))
+            made = made + len(ahead)
+            window = sum(columns(n) for n in ahead)
+            stores = len([job for job in jobs if todo[job] != [] and opens[job] < s and job not in sums]) + len(finished)
+            on_vector = min(stores, 0) if s >= 6 else 0
+            share = (2 * window + BANK * on_vector + 2 * columns(s) - 1000) // 3 // PACK // REP * REP
+            if side == "k":
+                share = min(share, count + 128)
+            rows = 2 * count * len(passes)
+            share = max(0, min(share, rows))
+            parts[s] = work.tile([P, 2 * columns(s)], BF16, name="parts", bufs=1, align_bytes=64)
+            times_amplitude(True, s, 0, share)
+            early = min(4, stores - on_vector)
+            for n in range(early):
+                store(s - 1, finished[0], False)
+            for n in ahead:
+                reduce_chunk(n)
+                trig(n)
+            for n in range(stores - on_vector - early):
+                store(s - 1, finished[0], False)
+            if s < 4 + 1:
+                group_x(s - 1)
+            if window or not 0:
+                times_amplitude(False, s, share, rows)
+            else:
+                times_amplitude(False, s, share, rows - count)
+                quantize("part%d_0" % s, parts[s][:, 0 : columns(s)])
+                similarity(s)
+                times_amplitude(False, s, rows - count, rows)
+            for n in range(on_vector):
+                store(s - 1, finished[0], True)
+            if s < 5 + 1:
+                quantize("x%d" % (s - 1 - 1), x_grp[s - 1 - 1][:])
                 pump()
-            if s == 1:
-                for i in range(1, 4):
-                    quantize("x%d" % i, x_grp[i][:])
-            quantize("chunk%d" % s, parts[s][:])
-            pump()
-            pending = [(job, similarity(job)) for job in products(s)]
-        for n, (job, bank) in enumerate(pending):
-            store(job, bank, n % 2 == 1)
+            for part in ((0, 1) if window or not 0 else (1,)):
+                quantize("part%d_%d" % (s, part), parts[s][:, part * columns(s) : (part + 1) * columns(s)])
+                similarity(s)
+        for n in range(len(finished)):
+            store(len(chunks), finished[0], n % 2 == 1)

@@ -21,9 +21,14 @@ P = 128
 PACK = 4
 BANK = 512
 PASSES = F // (P * PACK)
-REP = 32
+TURN = 256
+HALF = 256
+REPEAT = 32
 PHASE_BANKS = 4
-OTHER_BANKS = 3
+SPARE_BANKS = 3
+ITEM_EXTRA = 64
+LAST_ROWS = 96
+LAST_PIECES = 2
 TWO_PI = 2.0 * math.pi
 
 
@@ -38,93 +43,91 @@ def tile_fhrrbounditemsimilarity_kernel(tc, x, y_bytes, y_scale, w, role, a, c, 
         def kept(name, width, dtype):
             return keep.tile([P, width], dtype, name=name, align_bytes=64)
 
-        w_raw = [kept("w_raw%d" % g, PACK * BANK, BF16) for g in range(PASSES)]
-        x_raw = [kept("x_raw%d" % i, 2 * D, BF16) for i in range(4)]
-        y_raw = [kept("y_raw%d" % h, 4 * D, U8) for h in range(2)]
-
-        def load_w(g):
-            nc.sync.dma_start(
-                out=w_raw[g][:].rearrange("p (j f) -> p j f", j=PACK),
-                in_=w[:, g * BANK : (g + 1) * BANK].rearrange("(p j) f -> p j f", j=PACK),
-            )
-
-        def load_x(i):
-            nc.sync.dma_start(
-                out=x_raw[i][:].rearrange("p (b d) -> p b d", b=2),
-                in_=x[i * 256 : (i + 1) * 256, :].rearrange("(b p) d -> p b d", p=P),
-            )
-
-        def load_y(h):
-            nc.sync.dma_start(
-                out=y_raw[h][:].rearrange("p (b d) -> p b d", b=4),
-                in_=y_bytes[h * 512 : (h + 1) * 512, :].rearrange("(b p) d -> p b d", p=P),
-            )
-
-        load_w(0)
-        load_x(0)
-        load_y(0)
-        load_w(1)
-        load_y(1)
-        for i in range(1, 4):
-            load_x(i)
-
-        ident = kept("ident", P, F32)
-        make_identity(nc, ident[:])
+        w_raw = [[kept("w_raw%d_%d" % (g, half), PACK * HALF, BF16) for half in range(2)] for g in range(PASSES)]
+        x_raw = [kept("x_raw%d" % i, 2 * D, BF16) for i in range(Q // TURN)]
+        y_raw = [kept("y_raw%d" % h, 4 * D, U8) for h in range(K // BANK)]
         y_sc = kept("y_sc", PACK, F32)
-        nc.gpsimd.dma_start(out=y_sc[:], in_=y_scale.rearrange("o (p t) -> p (o t)", t=PACK))
-        vec16 = {}
-        for name, vec in (("role", role), ("a", a), ("c", c)):
-            vec16[name] = kept(name + "16", PASSES * PACK, BF16)
-            nc.gpsimd.dma_start(
+        vec16 = {name: kept(name + "16", PASSES * PACK, BF16) for name in ("role", "a", "c")}
+
+        def load_w(g, half):
+            lo = g * BANK + half * HALF
+            nc.sync.dma_start(
+                out=w_raw[g][half][:].rearrange("p (j f) -> p j f", j=PACK),
+                in_=w[:, lo : lo + HALF].rearrange("(p j) f -> p j f", j=PACK),
+            )
+
+        def load_rows(dst, src, first, count):
+            nc.sync.dma_start(
+                out=dst[:].rearrange("p (b d) -> p b d", d=D),
+                in_=src[first : first + count, :].rearrange("(b p) d -> p b d", p=P),
+            )
+
+        load_w(0, 0)
+        load_rows(x_raw[0], x, 0, TURN)
+        load_w(0, 1)
+        load_rows(y_raw[0], y_bytes, 0, BANK)
+        load_w(1, 0)
+        load_w(1, 1)
+        nc.sync.dma_start(out=y_sc[:], in_=y_scale.rearrange("o (p t) -> p (o t)", t=PACK))
+        for name, vec in (("a", a), ("c", c), ("role", role)):
+            nc.sync.dma_start(
                 out=vec16[name][:].rearrange("p (g t) -> p g t", t=PACK),
                 in_=vec.rearrange("(g p t) -> p g t", p=P, t=PACK),
             )
+        load_rows(y_raw[1], y_bytes, BANK, BANK)
+        for i in range(1, Q // TURN):
+            load_rows(x_raw[i], x, i * TURN, TURN)
 
+        ident = kept("ident", P, F32)
+        make_identity(nc, ident[:])
         ident16 = kept("ident16", P, BF16)
         make_identity(nc, ident16[:])
         amp_bank = psum.tile([P, BANK], F32, name="amp_bank")
 
+        free_banks = ["spare%d" % n for n in range(SPARE_BANKS)]
+        bank_of = {}
+
+        def take_bank(user):
+            bank_of[user] = free_banks.pop(0)
+            return psum.tile([P, BANK], F32, name=bank_of[user])
+
+        def give_bank(user):
+            free_banks.append(bank_of[user])
+
         w_grp = [kept("w_grp%d" % g, PACK * BANK, BF16) for g in range(PASSES)]
-        x_grp = [kept("x_grp%d" % i, PACK * 256, BF16) for i in range(4)]
-        y_wide = [kept("y_wide%d" % h, 4 * D, BF16) for h in range(2)]
-        y_grp = [kept("y_grp%d" % h, PACK * 512, BF16) for h in range(2)]
-        mx = {}
+        x_grp = [kept("x_grp%d" % i, PACK * TURN, BF16) for i in range(Q // TURN)]
+        y_wide = [kept("y_wide%d" % h, 4 * D, BF16) for h in range(K // BANK)]
+        y_grp = [kept("y_grp%d" % h, PACK * BANK, BF16) for h in range(K // BANK)]
+        quantised = {}
 
         def quantize(name, grouped):
             width = grouped.shape[1] // PACK
             codes = kept(name + "_codes", width, U32)
             scales = kept(name + "_scales", width, U8)
             nc.vector.quantize_mx(out=codes[:].bitcast(FP8X4), scales=scales[:], in_=grouped)
-            mx[name] = (codes, scales)
+            quantised[name] = (codes, scales)
 
         def operand(name, start, width):
-            codes, scales = mx[name]
+            codes, scales = quantised[name]
             return codes[:, start : start + width].bitcast(FP8X4), scales[:, start : start + width]
 
-        def group_w(g, copy):
+        def group_w(g, half, copy):
+            ms = slice(half * HALF // PACK, (half + 1) * HALF // PACK)
             copy(
-                out=w_grp[g][:].rearrange("p (t m j) -> p m t j", t=PACK, j=PACK),
-                in_=w_raw[g][:].rearrange("p (j m t) -> p m t j", j=PACK, t=PACK),
+                out=w_grp[g][:].rearrange("p (t m j) -> p m t j", t=PACK, j=PACK)[:, ms],
+                in_=w_raw[g][half][:].rearrange("p (j m t) -> p m t j", j=PACK, t=PACK),
             )
 
-        free_banks = ["other%d" % n for n in range(OTHER_BANKS)]
-        bank_number = {}
-
-        def take_bank(user):
-            bank_number[user] = free_banks.pop(0)
-            return psum.tile([P, BANK], F32, name=bank_number[user])
-
-        def give_bank(user):
-            free_banks.append(bank_number[user])
-
-        def turn(user, rows, first):
-            words = rows[:].bitcast(F32)
+        def turn(user, source, block):
+            words = source[:].bitcast(F32)
             bank = take_bank(user)
             for b in range(2):
                 for u in range(2):
-                    lo = (first + b) * 256
+                    lo = (block + b) * (D // 2)
                     nc.tensor.transpose(
-                        bank[:, u * 256 + b * P : u * 256 + (b + 1) * P], words[:, lo + u : lo + 256 : 2], ident[:]
+                        bank[:, u * TURN + b * P : u * TURN + (b + 1) * P],
+                        words[:, lo + u : lo + D // 2 : 2],
+                        ident[:],
                     )
             return bank
 
@@ -139,108 +142,104 @@ def tile_fhrrbounditemsimilarity_kernel(tc, x, y_bytes, y_scale, w, role, a, c, 
         def widen_y(h):
             nc.scalar.copy(out=y_wide[h][:], in_=y_raw[h][:].bitcast(FP8))
 
-        def scale_y(h, half, bank):
-            nc.vector.tensor_tensor(
-                out=y_grp[h][:, half * 1024 : (half + 1) * 1024].rearrange("p (r u e) -> p r u e", u=2, e=2),
-                in0=bank[:].bitcast(BF16).rearrange("p (u r e) -> p r u e", u=2, e=2),
-                in1=y_sc[:].rearrange("p (u e) -> p u e", u=2).unsqueeze(1).broadcast_to([P, 256, 2, 2]),
-                op=ALU.mult,
-            )
-            give_bank(("y", h, half))
+        def turn_y(h):
+            return [turn(("y", h, half), y_wide[h], 2 * half) for half in range(2)]
+
+        def scale_y(h, turned):
+            for half, bank in enumerate(turned):
+                dst = y_grp[h][:, half * PACK * TURN : (half + 1) * PACK * TURN]
+                nc.vector.tensor_tensor(
+                    out=dst.rearrange("p (r u e) -> p r u e", u=2, e=2),
+                    in0=bank[:].bitcast(BF16).rearrange("p (u r e) -> p r u e", u=2, e=2),
+                    in1=y_sc[:].rearrange("p (u e) -> p u e", u=2).unsqueeze(1).broadcast_to([P, TURN, 2, 2]),
+                    op=ALU.mult,
+                )
+                give_bank(("y", h, half))
 
         role32 = kept("role32", PASSES * PACK, F32)
-        rep = {"a": kept("a_rep", PASSES * REP * PACK, F32), "c": kept("c_rep", PASSES * REP * PACK, F32)}
+        repeated = {name: kept(name + "_rep", PASSES * REPEAT * PACK, F32) for name in ("a", "c")}
 
-        def spread(name):
+        def repeat(name):
+            by_pass = vec16[name][:].rearrange("p (g t) -> p g t", t=PACK)
             nc.vector.tensor_copy(
-                out=rep[name][:].rearrange("p (g r t) -> p g r t", g=PASSES, t=PACK),
-                in_=vec16[name][:].rearrange("p (g t) -> p g t", t=PACK).unsqueeze(2).broadcast_to([P, PASSES, REP, PACK]),
+                out=repeated[name][:].rearrange("p (g r t) -> p g r t", g=PASSES, t=PACK),
+                in_=by_pass.unsqueeze(2).broadcast_to([P, PASSES, REPEAT, PACK]),
             )
 
-        both = list(range(PASSES))
-        chunks = [("q", 0, 256, [g]) for g in both]
-        chunks = chunks + [("k", h * BANK, BANK, [g]) for h in range(2) for g in both]
-        for count in (256, 256, 128, 128):
-            chunks = chunks + [("q", 256 + sum(ch[2] for ch in chunks[6:]), count, both)]
+        all_passes = list(range(PASSES))
+        chunks = [("query", 0, TURN, [g]) for g in all_passes]
+        chunks = chunks + [("item", first, BANK, [g]) for first in range(0, K, BANK) for g in all_passes]
+        chunks = chunks + [("query", first, P, all_passes) for first in range(TURN, Q, P)]
 
         def columns(s):
             return PACK * chunks[s][2] * len(chunks[s][3])
 
-        banks = [(s, b) for s in range(len(chunks)) for b in range(columns(s) // BANK)]
-        first_bank = [banks.index((s, 0)) for s in range(len(chunks))]
-        phase = {}
-        turns = {}
-        reduced = {}
-        state = {"mm": 0, "done": 0}
+        fills = [(s, b) for s in range(len(chunks)) for b in range(columns(s) // BANK)]
+        phases, turns, reduced = {}, {}, {}
+        progress = {"filled": 0, "emptied": 0}
 
-        def bank_operands(n):
-            s, b = banks[n]
+        def fill_operands(n):
+            s, b = fills[n]
             side, first, count, passes = chunks[s]
-            if side == "q":
+            if side == "query":
                 g, j = divmod(b, count // P)
-                block = first // P + j
-                return "w%d" % passes[g], "x%d" % (block // 2), (block % 2) * P
+                i, start = divmod(first + j * P, TURN)
+                return "w%d" % passes[g], "x%d" % i, start
             return "w%d" % passes[0], "y%d" % (first // BANK), 0
 
-        def phase_matmul(n):
-            s, b = banks[n]
-            bank = psum.tile([P, BANK], F32, name="phase%d" % (n % PHASE_BANKS))
-            phase[n] = bank
-            weights, rows, start = bank_operands(n)
-            if chunks[s][0] == "q":
-                todo = [(t, bank[:, t * P : (t + 1) * P], P) for t in range(PACK)]
-            else:
-                todo = [(b, bank[:], BANK)]
-            for t, dst, width in todo:
-                lhsT, lhsT_scale = operand(weights, t * P, P)
-                rhs, rhs_scale = operand(rows, start, width)
-                nc.tensor.matmul_mx(out=dst, lhsT=lhsT, lhsT_scale=lhsT_scale, rhs=rhs, rhs_scale=rhs_scale,
-                                    start=True, stop=True)
-
-        def pump():
-            while state["mm"] < min(len(banks), state["done"] + PHASE_BANKS):
-                weights, rows, start = bank_operands(state["mm"])
-                if weights not in mx or rows not in mx:
+        def fill_banks():
+            while progress["filled"] < min(len(fills), progress["emptied"] + PHASE_BANKS):
+                n = progress["filled"]
+                weights, tokens, start = fill_operands(n)
+                if weights not in quantised or tokens not in quantised:
                     return
-                phase_matmul(state["mm"])
-                state["mm"] = state["mm"] + 1
+                s, b = fills[n]
+                phases[n] = psum.tile([P, BANK], F32, name="phase%d" % (n % PHASE_BANKS))
+                if chunks[s][0] == "query":
+                    slots = [(t, phases[n][:, t * P : (t + 1) * P], P) for t in range(PACK)]
+                else:
+                    slots = [(b, phases[n][:], BANK)]
+                for t, dst, width in slots:
+                    lhsT, lhsT_scale = operand(weights, t * P, P)
+                    rhs, rhs_scale = operand(tokens, start, width)
+                    nc.tensor.matmul_mx(
+                        out=dst, lhsT=lhsT, lhsT_scale=lhsT_scale, rhs=rhs, rhs_scale=rhs_scale, start=True, stop=True
+                    )
+                progress["filled"] = n + 1
 
-        def phase_view(n, ap):
-            if chunks[banks[n][0]][0] == "q":
-                return ap.rearrange("p (n t) -> p n t", t=PACK)
-            return ap
-
-        def bank_view(n):
-            if chunks[banks[n][0]][0] == "q":
-                return phase[n][:].rearrange("p (t n) -> p n t", t=PACK)
-            return phase[n][:]
+        def views(n, *ranges):
+            if chunks[fills[n][0]][0] == "item":
+                return [phases[n][:]] + list(ranges)
+            bank = phases[n][:].rearrange("p (t n) -> p n t", t=PACK)
+            return [bank] + [ap.rearrange("p (n t) -> p n t", t=PACK) for ap in ranges]
 
         def count_turns(n):
-            s, b = banks[n]
+            s, b = fills[n]
             side, first, count, passes = chunks[s]
             turns[n] = work.tile([P, BANK], I32, name="turns", bufs=3, align_bytes=64)
-            if side == "q":
-                nc.vector.tensor_scalar(out=phase_view(n, turns[n][:]), in0=bank_view(n), scalar1=1.0 / TWO_PI,
-                                        scalar2=None, op0=ALU.mult)
+            bank, dst = views(n, turns[n][:])
+            if side == "query":
+                nc.vector.tensor_scalar(out=dst, in0=bank, scalar1=1.0 / TWO_PI, scalar2=None, op0=ALU.mult)
             else:
                 col = passes[0] * PACK + b
-                nc.vector.tensor_scalar(out=turns[n][:], in0=bank_view(n), scalar1=role32[:, col : col + 1],
-                                        scalar2=1.0 / TWO_PI, op0=ALU.add, op1=ALU.mult)
+                nc.vector.tensor_scalar(
+                    out=dst, in0=bank, scalar1=role32[:, col : col + 1], scalar2=1.0 / TWO_PI, op0=ALU.add, op1=ALU.mult
+                )
 
         def subtract_turns(n):
-            s, b = banks[n]
+            s, b = fills[n]
             if b == 0:
                 reduced[s] = work.tile([P, columns(s)], F32, name="reduced", bufs=2, align_bytes=64)
-            nc.vector.scalar_tensor_tensor(
-                out=phase_view(n, reduced[s][:, b * BANK : (b + 1) * BANK]), in0=phase_view(n, turns[n][:]),
-                scalar=-TWO_PI, in1=bank_view(n), op0=ALU.mult, op1=ALU.add)
-            state["done"] = n + 1
-            pump()
-            if n + PHASE_BANKS >= len(banks):
+            bank, dst, whole = views(n, reduced[s][:, b * BANK : (b + 1) * BANK], turns[n][:])
+            nc.vector.scalar_tensor_tensor(out=dst, in0=whole, scalar=-TWO_PI, in1=bank, op0=ALU.mult, op1=ALU.add)
+            progress["emptied"] = n + 1
+            fill_banks()
+            if n + PHASE_BANKS >= len(fills):
                 free_banks.append("phase%d" % (n % PHASE_BANKS))
 
         def reduce_chunk(s):
-            lo, hi = first_bank[s], first_bank[s] + columns(s) // BANK
+            lo = fills.index((s, 0))
+            hi = lo + columns(s) // BANK
             count_turns(lo)
             for n in range(lo, hi):
                 if n + 1 < hi:
@@ -249,224 +248,230 @@ def tile_fhrrbounditemsimilarity_kernel(tc, x, y_bytes, y_scale, w, role, a, c, 
 
         trigs = {}
 
-        def trig(s):
+        def trig(s, bank_by_bank):
             side, first, count, passes = chunks[s]
             cosines = work.tile([P, columns(s)], F32, name="cosines", bufs=3, align_bytes=64)
             sines = work.tile([P, columns(s)], F32, name="sines", bufs=3, align_bytes=64)
             folded = work.tile([P, columns(s)], F32, name="folded", bufs=2, align_bytes=64)
             trigs[s] = (cosines, sines)
-            pieces = columns(s) // BANK
+            nbanks = columns(s) // BANK
 
-            def shifted(func, dst, lo, hi):
-                if side == "q":
-                    nc.scalar.activation(out=dst[:, lo * BANK : hi * BANK], in_=reduced[s][:, lo * BANK : hi * BANK], func=func)
+            def apply(func, dst, lo, hi):
+                if side == "query":
+                    cols = slice(lo * BANK, hi * BANK)
+                    nc.scalar.activation(out=dst[:, cols], in_=reduced[s][:, cols], func=func)
                     return
                 for t in range(lo, hi):
+                    cols = slice(t * BANK, (t + 1) * BANK)
                     col = passes[0] * PACK + t
-                    nc.scalar.activation(out=dst[:, t * BANK : (t + 1) * BANK],
-                                         in_=reduced[s][:, t * BANK : (t + 1) * BANK],
-                                         func=func, bias=role32[:, col : col + 1])
+                    nc.scalar.activation(
+                        out=dst[:, cols], in_=reduced[s][:, cols], func=func, bias=role32[:, col : col + 1]
+                    )
 
-            for b in range(pieces):
-                shifted(ACT.Abs, folded, b, b + 1)
-            if 1:
-                shifted(ACT.Sin, sines, 0, 1)
-            if side == "q":
-                nc.scalar.activation(out=cosines[:], in_=folded[:], func=ACT.Sin, scale=-1.0, bias=math.pi / 2)
-            else:
-                nc.scalar.activation(
-                    out=cosines[:].rearrange("p (m i t) -> p m t i", i=2, t=PACK),
-                    in_=folded[:].rearrange("p (t m i) -> p m t i", i=2, t=PACK),
-                    func=ACT.Sin, scale=-1.0, bias=math.pi / 2)
-            if pieces > 1:
-                shifted(ACT.Sin, sines, 1, pieces)
+            group = 1 if bank_by_bank else nbanks
+            for b in range(0, nbanks, group):
+                apply(ACT.Abs, folded, b, b + group)
+            apply(ACT.Sin, sines, 0, group)
+            src, dst = folded[:], cosines[:]
+            if side == "item":
+                src = src.rearrange("p (t m i) -> p m t i", i=2, t=PACK)
+                dst = dst.rearrange("p (m i t) -> p m t i", i=2, t=PACK)
+            nc.scalar.activation(out=dst, in_=src, func=ACT.Sin, scale=-1.0, bias=math.pi / 2)
+            if bank_by_bank:
+                apply(ACT.Sin, sines, 1, nbanks)
 
         parts = {}
 
-        def times_amplitude(on_gpsimd, s, lo, hi):
-            side, first, count, passes = chunks[s]
-            while lo < hi:
-                segment, token = divmod(lo, count)
-                part, g = divmod(segment, len(passes))
-                if token == 0 and g == 0 and hi - lo >= count * len(passes):
-                    groups, rows = len(passes), count
-                else:
-                    groups, rows = 1, min(count - token, hi - lo)
-                product(on_gpsimd, s, part, g, groups, token, token + rows)
-                lo = lo + groups * rows
+        def new_parts(s, name):
+            parts[s] = work.tile([P, 2 * columns(s)], BF16, name=name, bufs=1, align_bytes=64)
 
-        def product(on_gpsimd, s, part, g, groups, lo, hi):
+        def product(on_gpsimd, s, part, g, npasses, lo, hi):
             side, first, count, passes = chunks[s]
-            width = columns(s)
-            run = REP * PACK
-            cols = slice(g * count * PACK, (g + groups) * count * PACK)
-            dst = parts[s][:, part * width : (part + 1) * width][:, cols]
+            cols = slice(g * count * PACK, (g + npasses) * count * PACK)
+            dst = parts[s][:, part * columns(s) : (part + 1) * columns(s)][:, cols]
             src = trigs[s][part][:, cols]
-            engine = nc.gpsimd if on_gpsimd else nc.vector
-            name = "a" if side == "q" else "c"
-            amp = rep[name][:, passes[g] * run : (passes[g] + groups) * run].rearrange("p (g f) -> p g f", g=groups)
-            if not on_gpsimd:
-                base = (0 if side == "q" else PASSES * PACK) + passes[g] * PACK
-                amp = amp_bank[:, base : base + groups * PACK].rearrange("p (g f) -> p g f", g=groups)
-            if side == "k" and part == 1:
+            if on_gpsimd:
+                engine, run = nc.gpsimd, REPEAT * PACK
+                amp = repeated["a" if side == "query" else "c"][:, passes[g] * run : (passes[g] + npasses) * run]
+            else:
+                engine, run = nc.vector, PACK
+                base = (0 if side == "query" else PASSES * PACK) + passes[g] * PACK
+                amp = amp_bank[:, base : base + npasses * PACK]
+            amp = amp.rearrange("p (g f) -> p g f", g=npasses)
+            if side == "item" and part == 1:
                 pairs = slice(lo // 2, hi // 2)
                 engine.tensor_tensor(
                     out=dst.rearrange("p (m i t) -> p m t i", i=2, t=PACK)[:, pairs],
                     in0=src.rearrange("p (t m i) -> p m t i", i=2, t=PACK)[:, pairs],
                     in1=amp[:, 0, 0:PACK].unsqueeze(1).unsqueeze(3).broadcast_to([P, (hi - lo) // 2, PACK, 2]),
-                    op=ALU.mult)
+                    op=ALU.mult,
+                )
                 return
-            inner = run if on_gpsimd else PACK
 
-            def view(ap):
-                ap = ap.rearrange("p (g f) -> p g f", g=groups)[:, :, lo * PACK : hi * PACK]
-                return ap.rearrange("p g (n f) -> p g n f", f=inner)
+            def in_runs(ap):
+                ap = ap.rearrange("p (g f) -> p g f", g=npasses)[:, :, lo * PACK : hi * PACK]
+                return ap.rearrange("p g (n f) -> p g n f", f=run)
 
             engine.tensor_tensor(
-                out=view(dst), in0=view(src),
-                in1=amp.unsqueeze(2).broadcast_to([P, groups, (hi - lo) * PACK // inner, inner]),
-                op=ALU.mult)
+                out=in_runs(dst),
+                in0=in_runs(src),
+                in1=amp.unsqueeze(2).broadcast_to([P, npasses, (hi - lo) * PACK // run, run]),
+                op=ALU.mult,
+            )
 
-        def piece(side, token, part, g, width):
-            for s, (side_s, first, count, passes) in enumerate(chunks):
-                if side_s == side and first <= token < first + count and g in passes:
-                    name = "part%d_%d" % (s, part)
-                    if name in mx:
-                        return operand(name, passes.index(g) * count + token - first, width)
-            return None
+        def products(on_gpsimd, s, lo, hi):
+            side, first, count, passes = chunks[s]
+            while lo < hi:
+                segment, token = divmod(lo, count)
+                part, g = divmod(segment, len(passes))
+                if token == 0 and g == 0 and hi - lo >= count * len(passes):
+                    npasses, ntokens = len(passes), count
+                else:
+                    npasses, ntokens = 1, min(count - token, hi - lo)
+                product(on_gpsimd, s, part, g, npasses, token, token + ntokens)
+                lo = lo + npasses * ntokens
 
-        def step_of(side, token, g):
+        def quantize_part(s, part):
+            quantize("part%d_%d" % (s, part), parts[s][:, part * columns(s) : (part + 1) * columns(s)])
+
+        def chunk_of(side, token, g):
             return [s for s, ch in enumerate(chunks) if ch[0] == side and ch[1] <= token < ch[1] + ch[2] and g in ch[3]][0]
 
-        jobs = [(row, col) for row in range(0, Q, P) for col in range(0, K, BANK)]
-        opens = {job: max(step_of("q", job[0], 0), step_of("k", job[1], PASSES - 1)) for job in jobs}
-        todo = {job: [(part, g) for part in (1, 0) for g in both] for job in jobs}
+        def part_operand(side, token, part, g, width):
+            s = chunk_of(side, token, g)
+            name = "part%d_%d" % (s, part)
+            if name not in quantised:
+                return None
+            return operand(name, chunks[s][3].index(g) * chunks[s][2] + token - chunks[s][1], width)
+
+        tiles = [(row, col) for row in range(0, Q, P) for col in range(0, K, BANK)]
+        last_chunk = {
+            (row, col): max(chunk_of("query", row, PASSES - 1), chunk_of("item", col, PASSES - 1)) for row, col in tiles
+        }
+        missing = {tile: [(part, g) for part in (1, 0) for g in all_passes] for tile in tiles}
         sums = {}
         finished = []
 
         def similarity(s):
-            for job in jobs:
-                for part, g in [(part, g) for part in (1, 0) for g in both]:
-                    if opens[job] > s or (part, g) not in todo[job]:
-                        continue
-                    left, right = piece("q", job[0], part, g, P), piece("k", job[1], part, g, BANK)
+            for tile in tiles:
+                if last_chunk[tile] != s:
+                    continue
+                for part, g in list(missing[tile]):
+                    left = part_operand("query", tile[0], part, g, P)
+                    right = part_operand("item", tile[1], part, g, BANK)
                     if left is None or right is None:
                         continue
-                    start = job not in sums
-                    if start and not free_banks:
-                        continue
-                    if start:
-                        sums[job] = take_bank(job)
-                    todo[job].remove((part, g))
-                    nc.tensor.matmul_mx(out=sums[job][:], lhsT=left[0], lhsT_scale=left[1], rhs=right[0], rhs_scale=right[1],
-                                        start=start, stop=not todo[job])
-                    if not todo[job]:
-                        finished.append(job)
+                    opening = tile not in sums
+                    if opening:
+                        sums[tile] = take_bank(tile)
+                    missing[tile].remove((part, g))
+                    nc.tensor.matmul_mx(
+                        out=sums[tile][:], lhsT=left[0], lhsT_scale=left[1], rhs=right[0], rhs_scale=right[1],
+                        start=opening, stop=not missing[tile],
+                    )
+                if not missing[tile]:
+                    finished.append(tile)
 
-        def store(s, job, on_vector):
-            row, col = job
-            result = work.tile([P, BANK], F32, name="result", bufs=4, align_bytes=64)
-            if on_vector:
-                nc.vector.tensor_scalar(out=result[:], in0=sums[job][:], scalar1=1.0 / math.sqrt(F), scalar2=None, op0=ALU.mult)
-            else:
-                nc.scalar.activation(out=result[:], in_=sums[job][:], func=ACT.Copy, scale=1.0 / math.sqrt(F))
-            nc.sync.dma_start(out=out[row : row + P, col : col + BANK], in_=result[:])
-            give_bank(job)
-            finished.remove(job)
-            similarity(s)
+        def store(tile, on_vector, pieces):
+            row, col = tile
+            width = BANK // pieces
+            for lo in range(0, BANK, width):
+                result = work.tile([P, width], F32, name="result", bufs=8, align_bytes=64)
+                src = sums[tile][:, lo : lo + width]
+                if on_vector:
+                    nc.vector.tensor_scalar(
+                        out=result[:], in0=src, scalar1=1.0 / math.sqrt(F), scalar2=None, op0=ALU.mult
+                    )
+                else:
+                    nc.scalar.activation(out=result[:], in_=src, func=ACT.Copy, scale=1.0 / math.sqrt(F))
+                nc.sync.dma_start(out=out[row : row + P, col + lo : col + lo + width], in_=result[:])
+            give_bank(tile)
+
+        def store_finished():
+            for tile in finished:
+                store(tile, False, 1)
+            finished.clear()
 
         warm = kept("warm", 1, F32)
         nc.vector.memset(warm[:], 0.0)
         nc.scalar.activation(out=warm[:], in_=warm[:], func=ACT.Sin)
-        group_w(0, nc.vector.tensor_copy)
+        group_w(0, 0, nc.vector.tensor_copy)
         group_x(0)
+        group_w(0, 1, nc.vector.tensor_copy)
         widen_y(0)
         quantize("w0", w_grp[0][:])
         quantize("x0", x_grp[0][:])
-        pump()
-        y_banks = [turn(("y", 0, half), y_wide[0], 2 * half) for half in range(2)]
-        group_w(1, nc.scalar.copy)
+        fill_banks()
+        turned = turn_y(0)
+        group_w(1, 0, nc.vector.tensor_copy)
+        group_w(1, 1, nc.scalar.copy)
         reduce_chunk(0)
-        scale_y(0, 0, y_banks[0])
-        scale_y(0, 1, y_banks[1])
+        scale_y(0, turned)
         quantize("w1", w_grp[1][:])
-        pump()
-        trig(0)
+        fill_banks()
+        trig(0, True)
         widen_y(1)
         quantize("y0", y_grp[0][:])
-        pump()
+        fill_banks()
         for n, name in enumerate(("a", "c")):
-            nc.tensor.matmul(out=amp_bank[:, n * PASSES * PACK : (n + 1) * PASSES * PACK], lhsT=ident16[:],
-                             rhs=vec16[name][:], start=True, stop=True)
+            nc.tensor.matmul(
+                out=amp_bank[:, n * PASSES * PACK : (n + 1) * PASSES * PACK],
+                lhsT=ident16[:], rhs=vec16[name][:], start=True, stop=True,
+            )
         nc.vector.tensor_copy(out=role32[:], in_=vec16["role"][:])
-        spread("a")
-        spread("c")
+        repeat("a")
+        repeat("c")
         reduce_chunk(1)
-        trig(1)
-        y_banks = [turn(("y", 1, half), y_wide[1], 2 * half) for half in range(2)]
-        parts[0] = work.tile([P, 2 * columns(0)], BF16, name="parts_first", bufs=1, align_bytes=64)
-        times_amplitude(True, 0, 0, 2 * chunks[0][2])
+        trig(1, True)
+        turned = turn_y(1)
+        new_parts(0, "parts_first")
+        products(True, 0, 0, 2 * TURN)
         reduce_chunk(2)
-        trig(2)
-        parts[1] = work.tile([P, 2 * columns(1)], BF16, name="parts_second", bufs=1, align_bytes=64)
-        times_amplitude(True, 1, 0, 2 * chunks[1][2])
-        made = 3
-        if 1:
-            parts[2] = work.tile([P, 2 * columns(2)], BF16, name="parts", bufs=1, align_bytes=64)
-            times_amplitude(True, 2, 0, 512)
+        trig(2, True)
+        new_parts(1, "parts_second")
+        products(True, 1, 0, 2 * TURN)
+        new_parts(2, "parts")
+        products(True, 2, 0, BANK)
         reduce_chunk(3)
-        scale_y(1, 0, y_banks[0])
-        scale_y(1, 1, y_banks[1])
-        trig(3)
-        group_x(1)
-        if 1:
-            times_amplitude(False, 2, 512, 2 * BANK)
+        scale_y(1, turned)
+        trig(3, True)
+        for i in range(1, Q // TURN):
+            group_x(i)
+        products(False, 2, BANK, 2 * BANK)
         quantize("y1", y_grp[1][:])
-        pump()
-        for done in range(2 + 1):
-            for part in (0, 1):
-                quantize("part%d_%d" % (done, part), parts[done][:, part * columns(done) : (part + 1) * columns(done)])
-        made = 4
+        fill_banks()
+        for s in range(3):
+            for part in range(2):
+                quantize_part(s, part)
 
-        for s in range(2 + 1, len(chunks)):
+        next_chunk, next_x = 4, 1
+        for s in range(3, len(chunks)):
             side, first, count, passes = chunks[s]
-            lag = 1 if s < 6 else 2
-            ahead = list(range(made, min(s + lag + 1, len(chunks))))
-            made = made + len(ahead)
-            window = sum(columns(n) for n in ahead)
-            stores = len([job for job in jobs if todo[job] != [] and opens[job] < s and job not in sums]) + len(finished)
-            on_vector = min(stores, 0) if s >= 6 else 0
-            share = (2 * window + BANK * on_vector + 2 * columns(s) - 1000) // 3 // PACK // REP * REP
-            if side == "k":
-                share = min(share, count + 128)
+            distance = 1 if s + 1 < len(chunks) and chunks[s + 1][0] == "item" else 2
+            ahead = list(range(next_chunk, min(s + distance + 1, len(chunks))))
+            next_chunk = next_chunk + len(ahead)
             rows = 2 * count * len(passes)
-            share = max(0, min(share, rows))
-            parts[s] = work.tile([P, 2 * columns(s)], BF16, name="parts", bufs=1, align_bytes=64)
-            times_amplitude(True, s, 0, share)
-            early = min(4, stores - on_vector)
-            for n in range(early):
-                store(s - 1, finished[0], False)
+            if not ahead:
+                share = LAST_ROWS
+            elif side == "item":
+                share = rows // 2 + ITEM_EXTRA
+            else:
+                share = rows // 2
+            new_parts(s, "parts")
+            products(True, s, 0, share)
+            if next_chunk < len(chunks):
+                store_finished()
             for n in ahead:
                 reduce_chunk(n)
-                trig(n)
-            for n in range(stores - on_vector - early):
-                store(s - 1, finished[0], False)
-            if s < 4 + 1:
-                group_x(s - 1)
-            if window or not 0:
-                times_amplitude(False, s, share, rows)
-            else:
-                times_amplitude(False, s, share, rows - count)
-                quantize("part%d_0" % s, parts[s][:, 0 : columns(s)])
+                trig(n, chunks[n][0] == "item")
+            store_finished()
+            products(False, s, share, rows)
+            if next_x < Q // TURN:
+                quantize("x%d" % next_x, x_grp[next_x][:])
+                fill_banks()
+                next_x = next_x + 1
+            for part in range(2):
+                quantize_part(s, part)
                 similarity(s)
-                times_amplitude(False, s, rows - count, rows)
-            for n in range(on_vector):
-                store(s - 1, finished[0], True)
-            if s < 5 + 1:
-                quantize("x%d" % (s - 1 - 1), x_grp[s - 1 - 1][:])
-                pump()
-            for part in ((0, 1) if window or not 0 else (1,)):
-                quantize("part%d_%d" % (s, part), parts[s][:, part * columns(s) : (part + 1) * columns(s)])
-                similarity(s)
-        for n in range(len(finished)):
-            store(len(chunks), finished[0], n % 2 == 1)
+        for n, tile in enumerate(finished):
+            store(tile, n == 1, LAST_PIECES)

import math
from contextlib import ExitStack

import concourse.mybir as mybir
from concourse.masks import make_identity

Q, K, D, F = 1024, 1024, 512, 1024
FLOPS = 2 * (Q * D * F + K * D * F + 2 * Q * K * F)

F32 = mybir.dt.float32
BF16 = mybir.dt.bfloat16
I32 = mybir.dt.int32
U32 = mybir.dt.uint32
U8 = mybir.dt.uint8
FP8 = mybir.dt.float8_e4m3fn
FP8X4 = mybir.dt.float8_e4m3fn_x4
ALU = mybir.AluOpType
ACT = mybir.ActivationFunctionType

P = 128
PACK = 4
BANK = 512
PASSES = F // (P * PACK)
TURN = 256
HALF = 256
REPEAT = 32
PHASE_BANKS = 4
SPARE_BANKS = 3
ITEM_EXTRA = 64
LAST_ROWS = 96
LAST_PIECES = 2
TWO_PI = 2.0 * math.pi


def tile_fhrrbounditemsimilarity_kernel(tc, x, y_bytes, y_scale, w, role, a, c, out):
    nc = tc.nc
    with ExitStack() as ctx:
        keep = ctx.enter_context(tc.tile_pool(name="keep", bufs=1))
        work = ctx.enter_context(tc.tile_pool(name="work", bufs=2))
        psum = ctx.enter_context(tc.psum_pool(name="psum", bufs=1))
        ctx.enter_context(tc.manual_schedule())

        def kept(name, width, dtype):
            return keep.tile([P, width], dtype, name=name, align_bytes=64)

        w_raw = [[kept("w_raw%d_%d" % (g, half), PACK * HALF, BF16) for half in range(2)] for g in range(PASSES)]
        x_raw = [kept("x_raw%d" % i, 2 * D, BF16) for i in range(Q // TURN)]
        y_raw = [kept("y_raw%d" % h, 4 * D, U8) for h in range(K // BANK)]
        y_sc = kept("y_sc", PACK, F32)
        vec16 = {name: kept(name + "16", PASSES * PACK, BF16) for name in ("role", "a", "c")}

        def load_w(g, half):
            lo = g * BANK + half * HALF
            nc.sync.dma_start(
                out=w_raw[g][half][:].rearrange("p (j f) -> p j f", j=PACK),
                in_=w[:, lo : lo + HALF].rearrange("(p j) f -> p j f", j=PACK),
            )

        def load_rows(dst, src, first, count):
            nc.sync.dma_start(
                out=dst[:].rearrange("p (b d) -> p b d", d=D),
                in_=src[first : first + count, :].rearrange("(b p) d -> p b d", p=P),
            )

        load_w(0, 0)
        load_rows(x_raw[0], x, 0, TURN)
        load_w(0, 1)
        load_rows(y_raw[0], y_bytes, 0, BANK)
        load_w(1, 0)
        load_w(1, 1)
        nc.sync.dma_start(out=y_sc[:], in_=y_scale.rearrange("o (p t) -> p (o t)", t=PACK))
        for name, vec in (("a", a), ("c", c), ("role", role)):
            nc.sync.dma_start(
                out=vec16[name][:].rearrange("p (g t) -> p g t", t=PACK),
                in_=vec.rearrange("(g p t) -> p g t", p=P, t=PACK),
            )
        load_rows(y_raw[1], y_bytes, BANK, BANK)
        for i in range(1, Q // TURN):
            load_rows(x_raw[i], x, i * TURN, TURN)

        ident = kept("ident", P, F32)
        make_identity(nc, ident[:])
        ident16 = kept("ident16", P, BF16)
        make_identity(nc, ident16[:])
        amp_bank = psum.tile([P, BANK], F32, name="amp_bank")

        free_banks = ["spare%d" % n for n in range(SPARE_BANKS)]
        bank_of = {}

        def take_bank(user):
            bank_of[user] = free_banks.pop(0)
            return psum.tile([P, BANK], F32, name=bank_of[user])

        def give_bank(user):
            free_banks.append(bank_of[user])

        w_grp = [kept("w_grp%d" % g, PACK * BANK, BF16) for g in range(PASSES)]
        x_grp = [kept("x_grp%d" % i, PACK * TURN, BF16) for i in range(Q // TURN)]
        y_wide = [kept("y_wide%d" % h, 4 * D, BF16) for h in range(K // BANK)]
        y_grp = [kept("y_grp%d" % h, PACK * BANK, BF16) for h in range(K // BANK)]
        quantised = {}

        def quantize(name, grouped):
            width = grouped.shape[1] // PACK
            codes = kept(name + "_codes", width, U32)
            scales = kept(name + "_scales", width, U8)
            nc.vector.quantize_mx(out=codes[:].bitcast(FP8X4), scales=scales[:], in_=grouped)
            quantised[name] = (codes, scales)

        def operand(name, start, width):
            codes, scales = quantised[name]
            return codes[:, start : start + width].bitcast(FP8X4), scales[:, start : start + width]

        def group_w(g, half, copy):
            ms = slice(half * HALF // PACK, (half + 1) * HALF // PACK)
            copy(
                out=w_grp[g][:].rearrange("p (t m j) -> p m t j", t=PACK, j=PACK)[:, ms],
                in_=w_raw[g][half][:].rearrange("p (j m t) -> p m t j", j=PACK, t=PACK),
            )

        def turn(user, source, block):
            words = source[:].bitcast(F32)
            bank = take_bank(user)
            for b in range(2):
                for u in range(2):
                    lo = (block + b) * (D // 2)
                    nc.tensor.transpose(
                        bank[:, u * TURN + b * P : u * TURN + (b + 1) * P],
                        words[:, lo + u : lo + D // 2 : 2],
                        ident[:],
                    )
            return bank

        def group_x(i):
            bank = turn(("x", i), x_raw[i], 0)
            nc.scalar.copy(
                out=x_grp[i][:].bitcast(F32).rearrange("p (r u) -> p r u", u=2),
                in_=bank[:].rearrange("p (u r) -> p r u", u=2),
            )
            give_bank(("x", i))

        def widen_y(h):
            nc.scalar.copy(out=y_wide[h][:], in_=y_raw[h][:].bitcast(FP8))

        def turn_y(h):
            return [turn(("y", h, half), y_wide[h], 2 * half) for half in range(2)]

        def scale_y(h, turned):
            for half, bank in enumerate(turned):
                dst = y_grp[h][:, half * PACK * TURN : (half + 1) * PACK * TURN]
                nc.vector.tensor_tensor(
                    out=dst.rearrange("p (r u e) -> p r u e", u=2, e=2),
                    in0=bank[:].bitcast(BF16).rearrange("p (u r e) -> p r u e", u=2, e=2),
                    in1=y_sc[:].rearrange("p (u e) -> p u e", u=2).unsqueeze(1).broadcast_to([P, TURN, 2, 2]),
                    op=ALU.mult,
                )
                give_bank(("y", h, half))

        role32 = kept("role32", PASSES * PACK, F32)
        repeated = {name: kept(name + "_rep", PASSES * REPEAT * PACK, F32) for name in ("a", "c")}

        def repeat(name):
            by_pass = vec16[name][:].rearrange("p (g t) -> p g t", t=PACK)
            nc.vector.tensor_copy(
                out=repeated[name][:].rearrange("p (g r t) -> p g r t", g=PASSES, t=PACK),
                in_=by_pass.unsqueeze(2).broadcast_to([P, PASSES, REPEAT, PACK]),
            )

        all_passes = list(range(PASSES))
        chunks = [("query", 0, TURN, [g]) for g in all_passes]
        chunks = chunks + [("item", first, BANK, [g]) for first in range(0, K, BANK) for g in all_passes]
        chunks = chunks + [("query", first, P, all_passes) for first in range(TURN, Q, P)]

        def columns(s):
            return PACK * chunks[s][2] * len(chunks[s][3])

        fills = [(s, b) for s in range(len(chunks)) for b in range(columns(s) // BANK)]
        phases, turns, reduced = {}, {}, {}
        progress = {"filled": 0, "emptied": 0}

        def fill_operands(n):
            s, b = fills[n]
            side, first, count, passes = chunks[s]
            if side == "query":
                g, j = divmod(b, count // P)
                i, start = divmod(first + j * P, TURN)
                return "w%d" % passes[g], "x%d" % i, start
            return "w%d" % passes[0], "y%d" % (first // BANK), 0

        def fill_banks():
            while progress["filled"] < min(len(fills), progress["emptied"] + PHASE_BANKS):
                n = progress["filled"]
                weights, tokens, start = fill_operands(n)
                if weights not in quantised or tokens not in quantised:
                    return
                s, b = fills[n]
                phases[n] = psum.tile([P, BANK], F32, name="phase%d" % (n % PHASE_BANKS))
                if chunks[s][0] == "query":
                    slots = [(t, phases[n][:, t * P : (t + 1) * P], P) for t in range(PACK)]
                else:
                    slots = [(b, phases[n][:], BANK)]
                for t, dst, width in slots:
                    lhsT, lhsT_scale = operand(weights, t * P, P)
                    rhs, rhs_scale = operand(tokens, start, width)
                    nc.tensor.matmul_mx(
                        out=dst, lhsT=lhsT, lhsT_scale=lhsT_scale, rhs=rhs, rhs_scale=rhs_scale, start=True, stop=True
                    )
                progress["filled"] = n + 1

        def views(n, *ranges):
            if chunks[fills[n][0]][0] == "item":
                return [phases[n][:]] + list(ranges)
            bank = phases[n][:].rearrange("p (t n) -> p n t", t=PACK)
            return [bank] + [ap.rearrange("p (n t) -> p n t", t=PACK) for ap in ranges]

        def count_turns(n):
            s, b = fills[n]
            side, first, count, passes = chunks[s]
            turns[n] = work.tile([P, BANK], I32, name="turns", bufs=3, align_bytes=64)
            bank, dst = views(n, turns[n][:])
            if side == "query":
                nc.vector.tensor_scalar(out=dst, in0=bank, scalar1=1.0 / TWO_PI, scalar2=None, op0=ALU.mult)
            else:
                col = passes[0] * PACK + b
                nc.vector.tensor_scalar(
                    out=dst, in0=bank, scalar1=role32[:, col : col + 1], scalar2=1.0 / TWO_PI, op0=ALU.add, op1=ALU.mult
                )

        def subtract_turns(n):
            s, b = fills[n]
            if b == 0:
                reduced[s] = work.tile([P, columns(s)], F32, name="reduced", bufs=2, align_bytes=64)
            bank, dst, whole = views(n, reduced[s][:, b * BANK : (b + 1) * BANK], turns[n][:])
            nc.vector.scalar_tensor_tensor(out=dst, in0=whole, scalar=-TWO_PI, in1=bank, op0=ALU.mult, op1=ALU.add)
            progress["emptied"] = n + 1
            fill_banks()
            if n + PHASE_BANKS >= len(fills):
                free_banks.append("phase%d" % (n % PHASE_BANKS))

        def reduce_chunk(s):
            lo = fills.index((s, 0))
            hi = lo + columns(s) // BANK
            count_turns(lo)
            for n in range(lo, hi):
                if n + 1 < hi:
                    count_turns(n + 1)
                subtract_turns(n)

        trigs = {}

        def trig(s, bank_by_bank):
            side, first, count, passes = chunks[s]
            cosines = work.tile([P, columns(s)], F32, name="cosines", bufs=3, align_bytes=64)
            sines = work.tile([P, columns(s)], F32, name="sines", bufs=3, align_bytes=64)
            folded = work.tile([P, columns(s)], F32, name="folded", bufs=2, align_bytes=64)
            trigs[s] = (cosines, sines)
            nbanks = columns(s) // BANK

            def apply(func, dst, lo, hi):
                if side == "query":
                    cols = slice(lo * BANK, hi * BANK)
                    nc.scalar.activation(out=dst[:, cols], in_=reduced[s][:, cols], func=func)
                    return
                for t in range(lo, hi):
                    cols = slice(t * BANK, (t + 1) * BANK)
                    col = passes[0] * PACK + t
                    nc.scalar.activation(
                        out=dst[:, cols], in_=reduced[s][:, cols], func=func, bias=role32[:, col : col + 1]
                    )

            group = 1 if bank_by_bank else nbanks
            for b in range(0, nbanks, group):
                apply(ACT.Abs, folded, b, b + group)
            apply(ACT.Sin, sines, 0, group)
            src, dst = folded[:], cosines[:]
            if side == "item":
                src = src.rearrange("p (t m i) -> p m t i", i=2, t=PACK)
                dst = dst.rearrange("p (m i t) -> p m t i", i=2, t=PACK)
            nc.scalar.activation(out=dst, in_=src, func=ACT.Sin, scale=-1.0, bias=math.pi / 2)
            if bank_by_bank:
                apply(ACT.Sin, sines, 1, nbanks)

        parts = {}

        def new_parts(s, name):
            parts[s] = work.tile([P, 2 * columns(s)], BF16, name=name, bufs=1, align_bytes=64)

        def product(on_gpsimd, s, part, g, npasses, lo, hi):
            side, first, count, passes = chunks[s]
            cols = slice(g * count * PACK, (g + npasses) * count * PACK)
            dst = parts[s][:, part * columns(s) : (part + 1) * columns(s)][:, cols]
            src = trigs[s][part][:, cols]
            if on_gpsimd:
                engine, run = nc.gpsimd, REPEAT * PACK
                amp = repeated["a" if side == "query" else "c"][:, passes[g] * run : (passes[g] + npasses) * run]
            else:
                engine, run = nc.vector, PACK
                base = (0 if side == "query" else PASSES * PACK) + passes[g] * PACK
                amp = amp_bank[:, base : base + npasses * PACK]
            amp = amp.rearrange("p (g f) -> p g f", g=npasses)
            if side == "item" and part == 1:
                pairs = slice(lo // 2, hi // 2)
                engine.tensor_tensor(
                    out=dst.rearrange("p (m i t) -> p m t i", i=2, t=PACK)[:, pairs],
                    in0=src.rearrange("p (t m i) -> p m t i", i=2, t=PACK)[:, pairs],
                    in1=amp[:, 0, 0:PACK].unsqueeze(1).unsqueeze(3).broadcast_to([P, (hi - lo) // 2, PACK, 2]),
                    op=ALU.mult,
                )
                return

            def in_runs(ap):
                ap = ap.rearrange("p (g f) -> p g f", g=npasses)[:, :, lo * PACK : hi * PACK]
                return ap.rearrange("p g (n f) -> p g n f", f=run)

            engine.tensor_tensor(
                out=in_runs(dst),
                in0=in_runs(src),
                in1=amp.unsqueeze(2).broadcast_to([P, npasses, (hi - lo) * PACK // run, run]),
                op=ALU.mult,
            )

        def products(on_gpsimd, s, lo, hi):
            side, first, count, passes = chunks[s]
            while lo < hi:
                segment, token = divmod(lo, count)
                part, g = divmod(segment, len(passes))
                if token == 0 and g == 0 and hi - lo >= count * len(passes):
                    npasses, ntokens = len(passes), count
                else:
                    npasses, ntokens = 1, min(count - token, hi - lo)
                product(on_gpsimd, s, part, g, npasses, token, token + ntokens)
                lo = lo + npasses * ntokens

        def quantize_part(s, part):
            quantize("part%d_%d" % (s, part), parts[s][:, part * columns(s) : (part + 1) * columns(s)])

        def chunk_of(side, token, g):
            return [s for s, ch in enumerate(chunks) if ch[0] == side and ch[1] <= token < ch[1] + ch[2] and g in ch[3]][0]

        def part_operand(side, token, part, g, width):
            s = chunk_of(side, token, g)
            name = "part%d_%d" % (s, part)
            if name not in quantised:
                return None
            return operand(name, chunks[s][3].index(g) * chunks[s][2] + token - chunks[s][1], width)

        tiles = [(row, col) for row in range(0, Q, P) for col in range(0, K, BANK)]
        last_chunk = {
            (row, col): max(chunk_of("query", row, PASSES - 1), chunk_of("item", col, PASSES - 1)) for row, col in tiles
        }
        missing = {tile: [(part, g) for part in (1, 0) for g in all_passes] for tile in tiles}
        sums = {}
        finished = []

        def similarity(s):
            for tile in tiles:
                if last_chunk[tile] != s:
                    continue
                for part, g in list(missing[tile]):
                    left = part_operand("query", tile[0], part, g, P)
                    right = part_operand("item", tile[1], part, g, BANK)
                    if left is None or right is None:
                        continue
                    opening = tile not in sums
                    if opening:
                        sums[tile] = take_bank(tile)
                    missing[tile].remove((part, g))
                    nc.tensor.matmul_mx(
                        out=sums[tile][:], lhsT=left[0], lhsT_scale=left[1], rhs=right[0], rhs_scale=right[1],
                        start=opening, stop=not missing[tile],
                    )
                if not missing[tile]:
                    finished.append(tile)

        def store(tile, on_vector, pieces):
            row, col = tile
            width = BANK // pieces
            for lo in range(0, BANK, width):
                result = work.tile([P, width], F32, name="result", bufs=8, align_bytes=64)
                src = sums[tile][:, lo : lo + width]
                if on_vector:
                    nc.vector.tensor_scalar(
                        out=result[:], in0=src, scalar1=1.0 / math.sqrt(F), scalar2=None, op0=ALU.mult
                    )
                else:
                    nc.scalar.activation(out=result[:], in_=src, func=ACT.Copy, scale=1.0 / math.sqrt(F))
                nc.sync.dma_start(out=out[row : row + P, col + lo : col + lo + width], in_=result[:])
            give_bank(tile)

        def store_finished():
            for tile in finished:
                store(tile, False, 1)
            finished.clear()

        warm = kept("warm", 1, F32)
        nc.vector.memset(warm[:], 0.0)
        nc.scalar.activation(out=warm[:], in_=warm[:], func=ACT.Sin)
        group_w(0, 0, nc.vector.tensor_copy)
        group_x(0)
        group_w(0, 1, nc.vector.tensor_copy)
        widen_y(0)
        quantize("w0", w_grp[0][:])
        quantize("x0", x_grp[0][:])
        fill_banks()
        turned = turn_y(0)
        group_w(1, 0, nc.vector.tensor_copy)
        group_w(1, 1, nc.scalar.copy)
        reduce_chunk(0)
        scale_y(0, turned)
        quantize("w1", w_grp[1][:])
        fill_banks()
        trig(0, True)
        widen_y(1)
        quantize("y0", y_grp[0][:])
        fill_banks()
        for n, name in enumerate(("a", "c")):
            nc.tensor.matmul(
                out=amp_bank[:, n * PASSES * PACK : (n + 1) * PASSES * PACK],
                lhsT=ident16[:], rhs=vec16[name][:], start=True, stop=True,
            )
        nc.vector.tensor_copy(out=role32[:], in_=vec16["role"][:])
        repeat("a")
        repeat("c")
        reduce_chunk(1)
        trig(1, True)
        turned = turn_y(1)
        new_parts(0, "parts_first")
        products(True, 0, 0, 2 * TURN)
        reduce_chunk(2)
        trig(2, True)
        new_parts(1, "parts_second")
        products(True, 1, 0, 2 * TURN)
        new_parts(2, "parts")
        products(True, 2, 0, BANK)
        reduce_chunk(3)
        scale_y(1, turned)
        trig(3, True)
        for i in range(1, Q // TURN):
            group_x(i)
        products(False, 2, BANK, 2 * BANK)
        quantize("y1", y_grp[1][:])
        fill_banks()
        for s in range(3):
            for part in range(2):
                quantize_part(s, part)

        next_chunk, next_x = 4, 1
        for s in range(3, len(chunks)):
            side, first, count, passes = chunks[s]
            distance = 1 if s + 1 < len(chunks) and chunks[s + 1][0] == "item" else 2
            ahead = list(range(next_chunk, min(s + distance + 1, len(chunks))))
            next_chunk = next_chunk + len(ahead)
            rows = 2 * count * len(passes)
            if not ahead:
                share = LAST_ROWS
            elif side == "item":
                share = rows // 2 + ITEM_EXTRA
            else:
                share = rows // 2
            new_parts(s, "parts")
            products(True, s, 0, share)
            if next_chunk < len(chunks):
                store_finished()
            for n in ahead:
                reduce_chunk(n)
                trig(n, chunks[n][0] == "item")
            store_finished()
            products(False, s, share, rows)
            if next_x < Q // TURN:
                quantize("x%d" % next_x, x_grp[next_x][:])
                fill_banks()
                next_x = next_x + 1
            for part in range(2):
                quantize_part(s, part)
                similarity(s)
        for n, tile in enumerate(finished):
            store(tile, n == 1, LAST_PIECES)
